import numpy as np, ml_dtypes
CORES = [3,7,11,15,131,135,139,143]
N = 8
import mx_ref
BF = ml_dtypes.bfloat16
def gentries(a):
    return np.ascontiguousarray(a.reshape(8, 16, -1).transpose(0, 2, 1)).reshape(8, -1)
def gtable(e):
    e = np.asarray(e); return np.ascontiguousarray(e.reshape(8, -1, 16).transpose(0, 2, 1)).reshape(128, -1).astype(np.int32)
def gcols(t, e):
    v = np.concatenate([t.reshape(8, 16, -1, 4), np.zeros((8, 16, 1, 4), BF)], axis=2)
    return np.ascontiguousarray(np.stack([v[g][:, e[g]] for g in range(8)])).reshape(128, -1)
def gpick(z, e):
    return np.concatenate([z[16 * g:16 * g + 16][:, e[g]] for g in range(8)])
def tile(rs):
    return np.stack(rs, axis=2).reshape(128, -1).astype(BF)
def pick(q, e):
    c = np.concatenate([q[0].reshape(128, -1, 4), np.zeros((128, 1, 4), np.uint8)], axis=1); s = np.concatenate([q[1], np.ones((16, 1), np.uint8)], axis=1)
    return (np.ascontiguousarray(c[:, e].reshape(128, -1)), np.ascontiguousarray(s[:, e]))
def join(*qs):
    return (np.concatenate([q[0] for q in qs], axis=1), np.concatenate([q[1] for q in qs], axis=1))
def put(q, e, v):
    c, s = q[0].reshape(128, -1, 4).copy(), q[1].copy(); c[:, e] = v[0].reshape(128, -1, 4); s[:, e] = v[1]
    return (c.reshape(128, -1), s)
def pk(c, s):
    return (np.ascontiguousarray(c), mx_ref.live(s))
def emit(q):
    return q[0], q[1]
def packed(v, rng):
    q = [mx_ref.quantize(np.ascontiguousarray(v[r])) for r in range(N)]
    return np.stack([a for a, b in q]), np.stack([mx_ref.plane(b, rng) for a, b in q])
def values_of_codes():
    e, c = np.zeros((128, 128, 4), np.float32), np.zeros((128, 2, 4), np.uint8)
    e[np.arange(128), np.arange(128), 0] = 1
    c[:127, :, 0] = np.arange(256).reshape(2, 128).T[:127]
    return mx_ref.matmul(mx_ref.quantize(e.reshape(128, 512).astype(BF)), (c.reshape(128, 8), np.full((16, 2), 127, np.uint8))).T.reshape(-1).astype(np.float64)
CODE_VALUE, SCALE_VALUE = values_of_codes(), 2.0 ** (np.arange(256) - 127.0)
def decode(q):
    return (CODE_VALUE[q[0]].reshape(16, 8, -1, 4) * SCALE_VALUE[q[1]][:, None, :, None] + 0.0).reshape(128, -1).astype(np.float32)
def f(rng, *shape):
    return mx_ref.flush((rng.standard_normal(shape, dtype=np.float32) * np.exp2(rng.integers(-2, 3, shape[:-1] + (1,)))).astype(BF))
def wide(rng, *shape, cols=0):
    v = rng.standard_normal(shape, dtype=np.float32) * np.exp2(rng.integers(-12, 13, shape)).astype(np.float32)
    if cols: v *= np.repeat(np.exp2(rng.integers(-cols, cols + 1, shape[:-2] + (1, shape[-1] // 4))) * (rng.random(shape[:-2] + (1, shape[-1] // 4)) > 0.0625), 4, axis=-1).astype(np.float32)
    return mx_ref.flush(v.astype(BF))
C, K, A, R, SWEEPS = 288, 112, 64, 3, 4
def big(v):
    v = v.astype(np.float32)
    v[np.abs(v) < np.float32(2.0 ** -16)] = 0
    return v.astype(BF)
def numbers_of(rng):
    return {"x": big(f(rng, N, 128, 4 * C)), "u": np.array(f(rng, N, 128, 512)), "v": np.array(f(rng, N, 128, 512))}
def stored(t):
    return np.stack([gtable(np.clip(t[r], 0, C - 1)) for r in range(N)])
def received(rng):
    return stored(np.arange(C) + rng.integers(-6, 26, (N, 8, C)))
def give(rng, w):
    c, s = packed(np.ascontiguousarray(w).reshape(N, 128, 2048), rng)
    return {"wc": c, "ws": s}
def weights(rng, still=[]):
    w = np.array(mx_ref.flush((rng.standard_normal((N, 128, 2048), dtype=np.float32) * np.float32(0.25)).astype(BF))).reshape(N, 8, 16, 4, 8, 16, 4)
    for i in still:
        w[:, :, i] = 0
        w[:, :, :, :, :, i] = 0
    return give(rng, w)
def setup_inputs(rng):
    return {**numbers_of(rng), "rv": received(rng), **weights(rng)}
def setup_inputs_ties(rng):
    d = numbers_of(rng)
    x = d["x"].reshape(N, 8, 16, C, 4)
    x[:, :, 0] = 0
    x[:, :, 8] = 0
    x[:, :, 0, :, 0] = rng.integers(0, 3, (N, 8, C)).astype(np.float32).astype(BF)
    x[:, :, 8, :, 0] = rng.integers(-1, 2, (N, 8, C)).astype(np.float32).astype(BF)
    u = d["u"].reshape(N, 128, 128, 4)
    u[:, :, ::8] = 0
    o = rng.permutation(N)
    for r in range(N):
        for h in range(0, 128, 16):
            u[r, h, h, 0] = 0.0 if r == o[0] else -1.0 if r == o[1] else 1.0
            u[r, h + 8, h + 8, 0] = 1.0
    t = np.arange(C) + rng.integers(-6, 26, (N, 8, C))
    g = rng.integers(8)
    t[o[0] - 1, g - 1] = 21
    t[o[0], g, C - 1] = 1
    x[o[0], g, 8, C - 1, 0] = 1.0
    return {"x": x.reshape(N, 128, 4 * C), "u": u.reshape(N, 128, 512), "v": d["v"], "rv": stored(t), **weights(rng, [0, 8])}
def setup_inputs_near(rng):
    d = numbers_of(rng)
    x = d["x"].astype(np.float32).reshape(N, 8, 16, C, 4)
    x[:, :, 0] = 0
    x[:, :, 8:] = 0
    x[:, :, 0, :, 0] = rng.integers(0, 2, (N, 8, C)) * 2.0 - 1.0
    s = rng.integers(0, 16, (N, 8, C))
    t = rng.integers(-1, 2, (N, 8, C))
    x[:, :, 8] = ((s[:, :, :, None] >> np.arange(4)) & 1) * np.exp2(np.arange(4) - 23.0)
    x[:, :, 11, :, 0] = 2.0 ** -10
    x[:, :, 12, :, 0] = t * 2.0 ** -10
    u = d["u"].reshape(N, 128, 128, 4)
    u[:, :, ::8] = 0
    u[:, :, 8::16] = 0
    o = rng.permutation(N) % 2
    for r in range(N):
        if o[r] == 1:
            x[r, :, 8:] = 0
            x[r, :, 8, :, 0] = (s[r] - 8) * 2.0 ** -28
            x[r, :, 12, :, 0] = t[r] * 2.0 ** -28
            x[r, :, 13, :, 0] = rng.integers(0, 2, (8, C)) * 1.125 * 2.0 ** -28
            for g in rng.permutation(8)[:4]: x[r, g, 8, rng.integers(C), 0] = 2.0 ** 20 * rng.choice([-1.0, 1.0])
        for h in range(0, 128, 16):
            k = 2.0 ** -30 if o[r] == 1 else 1.0
            u[r, h + 12, h + 8, 0] = k
            if o[r] == 1:
                u[r, h + 8, h, 0] = k
                u[r, h + 13, h, 0] = k
                u[r, h + 13, h + 8, 0] = k
            else:
                u[r, h, h, 0] = k
                u[r, h + 8, h] = k
                u[r, h + 11, h, 0] = k
    return {"x": x.reshape(N, 128, 4 * C).astype(BF), "u": u.reshape(N, 128, 512), "v": d["v"], "rv": received(rng), **weights(rng, [0, 8, 9, 10, 11, 12, 13, 14, 15])}
def setup_inputs_chains(rng):
    d = numbers_of(rng)
    x = d["x"].reshape(N, 8, 16, C, 4)
    m = np.exp2(rng.integers(-12, -5, (N, 8, 8, C, 4))) * (1 + (2 * rng.integers(0, 64, (N, 8, 8, C, 4)) + 1) * 2.0 ** -7) * rng.choice([-1.0, 1.0], (N, 8, 8, C, 4))
    m[:, :, 3, :, 0] = 7.875 * rng.choice([-1.0, 1.0], (N, 8, C))
    x[:, :, :8] = m.astype(np.float32).astype(BF)
    x[:, :, 12] = 0
    x[:, :, 12, :, 0] = np.where(rng.random((N, 8, C)) < 0.0625, -1, 1).astype(np.float32).astype(BF)
    u = d["u"].reshape(N, 128, 128, 4)
    u[:, :, 8::16] = 0
    for h in range(0, 128, 16): u[:, h + 12, h + 8, 0] = 1
    t = np.arange(C) + np.zeros((N, 8, 1), np.int64)
    o = np.repeat(rng.permutation(4), 2) if N == 8 else np.concatenate([[1, 1], rng.permutation([0, 3])])
    o = np.roll(o, rng.integers(N))
    for r in range(N):
        if o[r] == 0: t[r] -= rng.integers(2, 5, (8, 1))
        elif o[r] == 1: t[r, rng.integers(8)] -= 21
        elif o[r] == 2: t[r] = C - 1
        else: t[r] += rng.integers(-30, 61, (8, C))
    return {"x": x.reshape(N, 128, 4 * C), "u": u.reshape(N, 128, 512), "v": d["v"], "rv": stored(t), **weights(rng, [12])}
def setup_inputs_ends(rng):
    d = numbers_of(rng)
    x = np.zeros((N, 8, 16, C, 4))
    u = d["u"].reshape(N, 128, 128, 4)
    w = np.full((N, 128, 2048), 0.25)
    t = np.full((N, 8, C), C - 1)
    i = np.arange(128)
    o = np.roll(np.concatenate([[3, 0], rng.permutation([1, 2])] * (N // 4)), rng.integers(N))
    for r in range(N):
        a = (0.9375 + 0.0625 * rng.integers(0, 2, (8, 16, C, 4))) * 2.0 ** 20
        c = (0.9375 + 0.0625 * rng.integers(0, 2, (128, 128, 4))) * 2.0 ** 30
        if o[r] < 2:
            x[r] = -a
            c[:, 8::16] *= 1.0 if o[r] == 0 else -1.0
            if o[r] == 1: t[r] = 0
            else:
                x[r] = -2.0 ** 20
                z = x[r].reshape(128, C, 4)
                z[:65:8] = 0
                z[:65:8, :, 0] = -((rng.permutation(C) >> np.arange(9)[:, None]) & 1) * np.exp2(11.0 + np.arange(9))[:, None]
                c[:, ::16] = 2.0 ** 30
                for g in rng.permutation(8)[:4]: c[:, 16 * g] *= -1.0
                c[:65:8, ::16, 0] = 2.0 ** 30
                w[r] = 0
                for b in range(4): w[r].reshape(128, 4, 128, 4)[i, b, i, b] = 128.0
            d["v"][r] = 2.0 ** 30
        elif o[r] == 2:
            e = np.arange(C) // 2
            x[r] = (a * rng.choice([-1.0, 1.0], (8, 1, C, 1)))[:, :, e]
            for g in range(8): c[np.arange(128) // 16 != g, 16 * g:16 * g + 16] = 0
            t[r, rng.permutation(8)[:4]] = 0
            d["v"][r] = (2.0 ** 30 * rng.choice([-1.0, 1.0], (128, 512))).astype(np.float32).astype(BF)
        else:
            x[r] = 2.0 ** -28
            c[:] = 2.0 ** -30
            w[r] = 2.0 ** -30
            d["v"][r] = 2.0 ** -30
        u[r] = c.astype(np.float32).astype(BF)
    return {"x": x.reshape(N, 128, 4 * C).astype(np.float32).astype(BF), "u": u.reshape(N, 128, 512), "v": d["v"], "rv": stored(t), **give(rng, w.astype(np.float32).astype(BF))}
def setup_inputs_spread(rng):
    d = setup_inputs(rng)
    d["x"] = big(np.clip(wide(rng, N, 128, 4 * C, cols=6).astype(np.float32), -2.0 ** 20, 2.0 ** 20))
    return d
def check_inputs(d):
    b = []
    for k, lo, hi in (("x", 2.0 ** -28, 2.0 ** 20), ("u", 2.0 ** -30, 2.0 ** 30), ("v", 2.0 ** -30, 2.0 ** 30)):
        a = np.abs(d[k].astype(np.float32))
        if not (np.isfinite(a).all() and ((a == 0) | (a >= lo) & (a <= hi)).all()): b.append("a value of " + k)
    if not ((d["rv"] >= 0) & (d["rv"] < C)).all(): b.append("an entry of rv")
    none, least, most = [emit(mx_ref.quantize(np.full((128, 16), k, np.float32).astype(BF)))[1][0, 0] for k in (0.0, 2.0 ** -30, 2.0 ** 30)]
    for r in range(N):
        if ((d["wc"][r] == 0x7F) | (d["wc"][r] == 0xFF)).any(): b.append("wc: a code that is no number")
        s = mx_ref.live(d["ws"][r])
        if ((s != none) & ((s < least) | (s > most))).any(): b.append("ws: a scale out of range")
        elif not (np.sum(np.abs(decode(pk(d["wc"][r], d["ws"][r])).astype(np.float64)).reshape(128, 512, 4), axis=(0, 2)) <= 128).all(): b.append("a column of W: its sizes")
    return b
def fall(p, b):
    for i in range(SWEEPS): p = np.minimum(p, np.roll(np.take_along_axis(b, p, axis=1), 1, axis=0))
    return p
def mean(a, b):
    return ((a.astype(np.float32) + b.astype(np.float32)) * np.float32(0.5)).astype(BF)
def reference(x, u, v, rv, wc, ws):
    qu = [mx_ref.quantize(u[r]) for r in range(N)]
    lay = [pk(wc[r], ws[r]) for r in range(N)]
    now = [x[r] for r in range(N)]
    p0 = np.zeros((8, 1), np.int64) + A + 2 * np.arange(K)
    lq = np.zeros((N, 8, K), np.float32)
    for t in range(R):
        own, order, bound, sent, line = [], [], [], [], []
        for r in range(N):
            q = mx_ref.quantize(now[r])
            own.append(decode(q).astype(BF))
            s = mx_ref.matmul(qu[r], q) + np.float32(0.0)
            o = np.argsort(-s[::16], axis=1, kind="stable")
            a = np.where(np.take_along_axis(s[8::16], o, axis=1) > 0, np.maximum(gentries(rv[r]) - 1, 0), C - 1)
            a = np.minimum.accumulate(a[:, ::-1], axis=1)[:, ::-1]
            order.append(o)
            bound.append(np.concatenate([a[:, 1:], np.full((8, 1), C - 1)], axis=1))
            line.append(fall(p0, bound[r]))
            sent.append(mx_ref.quantize(mean(gcols(own[r], np.take_along_axis(o, p0, axis=1)), gcols(own[r], np.take_along_axis(o, line[r], axis=1)))))
        for r in range(N):
            e = (r - 1) % N
            p = fall(line[e], bound[r])
            z = mx_ref.quantize(mean(decode(sent[e]), gcols(own[r], np.take_along_axis(order[r], p, axis=1))))
            hit = p[:, None, :] == np.arange(C)[:, None]
            low = np.zeros((8, C), np.int64)
            np.put_along_axis(low, order[r], np.where(hit.any(axis=2), np.argmax(hit, axis=2), K), axis=1)
            new = []
            for b in range(4):
                h = mx_ref.matmul(pick(lay[r], np.arange(128 * b, 128 * b + 128)), z) * np.float32(0.0625)
                new.append(own[r][:, b::4].astype(np.float32) + gpick(np.concatenate([h, np.zeros((128, 1), np.float32)], axis=1), low))
            now[r] = tile(new)
            lq[r] = p
    y = np.zeros((N, 128, C), np.float32)
    oc, osc = np.zeros((N, 128, 4 * C), np.uint8), np.zeros((N, 16, C), np.uint8)
    for r in range(N):
        q = mx_ref.quantize(now[r])
        y[r] = mx_ref.matmul(mx_ref.quantize(v[r]), q)
        oc[r], osc[r] = emit(q)
    return {"y": y, "lq": lq, "oc": oc, "osc": osc}

@@ -1,0 +1,467 @@
+from concourse.mybir import dt, AluOpType, ActivationFunctionType
+
+C, K, ROUNDS = 288, 112, 3
+NJ = C // 16
+UNIT = 1024.0
+TAGU = 4096.0
+CODE, F32, BF, I32, U16, U8 = "float8_e4m3fn_x4", "float32", "bfloat16", "int32", "uint16", "uint8"
+SLOTS = NJ + 1
+GW = 72 * SLOTS + 72
+CE, CC, CT, CZ = 0, 512, 640, 768
+
+SCRATCH = {"ps": ("psum", [128, 4096], F32)}
+
+
+def _sb(dtype, **names):
+    for n, w in names.items():
+        SCRATCH[n] = ("sbuf", [128, w], dtype)
+
+
+_sb(BF, x0=4 * C, X=1600, ub=512, vb=512, onesb=512, negb=512, cb=4 * 896, G=4 * GW, m4=C, m16=C, junk=4 * C,
+    FS=4 * C, A5=448, Et=512, Vt=512, DE=448, CV=448)
+_sb(F32, r4=C, r16=C, pflt=4, ic=C, I=C, r0c=K, dmy=K, cs=96, yl=NJ, ya=NJ, yb=NJ, yc=28, yd=28, a32=28, wr=C,
+    z=C, z1=144, z2=72, z3=36, own=24, OE=C, sg=C, sg2=C, Vr=C, Rs=NJ, R2=NJ, rk=NJ, PL=C, am=C, Bx=292, TAG=C,
+    T1=C, T2=C, T3=C, T4=C, Q1=C, Q2=C, Q3=C, Q4=C, P1=K, P2=K, P3=K, P4=K, w=K, w1=56, w2=28, FQ=448, eqn=K, kb=K, sel=K, lqf=K,
+    q0=K, q1=K, q4=K, yo=C)
+_sb(I32, rvt=NJ, pint=4, yi=NJ, oi1=C, oi=C, qi=K, qj=K)
+_sb(U16, rvl=NJ, sOM=16, lOE=NJ, lp18=NJ, lp7=8, lpo=8, Bo=K, Lo=8, lrv=NJ, lrq=8, lA=28, rkl=NJ, Bp=C, L1=NJ, L2=NJ, L3=NJ, L4=NJ, lo=72,
+    Pp=K, lE=28, lQ=28, lX=28, pls=40 * ROUNDS, pll=40 * ROUNDS)
+for _n, _w in [("qx", C), ("qu", 128), ("qv", 128), ("uo", 128), ("um", 128), ("wq", 512), ("cq", 896), ("gq", GW), ("vq", 128),
+               ("eq", 128 * ROUNDS), ("le", 128 * ROUNDS)]:
+    SCRATCH[_n] = ("sbuf", [128, _w], CODE)
+    SCRATCH[_n + "s"] = ("sbuf", [128, _w], U8)
+
+QS = {"v": "qsv", "a": "qsa", "t": "qst", "g": "qsg"}
+DS = ["dx", "du", "dv", "drv", "dwc", "dws", "dz", "dT1", "dL2", "dL3", "dLo", "dL4", "dP", "dlq", "doc", "dy"]
+SEMAPHORES = list(QS.values()) + DS + ["rl"] + ["ap%d" % _t for _t in range(ROUNDS)] + ["ae%d" % _t for _t in range(ROUNDS)]
+
+
+def make_tracker(g, T):
+    eng = {"v": g.vector, "a": g.scalar, "t": g.tensor, "g": g, "s": g.sync}
+    clk = {q: {} for q in eng}
+    cnt = {}
+    snaps = {}
+    acc = {}
+    seq, cur = [0], [None]
+
+    def hit(a, b):
+        if a[1] >= b[2] or b[1] >= a[2] or a[3] >= b[4] or b[3] >= a[4]:
+            return False
+        return not (a[5] == b[5] and a[5] > 1 and (a[3] - b[3]) % a[5])
+
+    def bank(r):
+        return (r[0], 0, 128, r[3] // 512 * 512, (r[4] + 511) // 512 * 512, 1) if r[0] == "ps" else r
+
+    def merge(q, sem, val):
+        own = clk[q]
+        own[sem] = max(own.get(sem, 0), val)
+        for v, s in snaps.get(sem, []):
+            if v <= val:
+                for a, b in s.items():
+                    own[a] = max(own.get(a, 0), b)
+
+    def emit(q, call, outs, ins, dma=None, remote=False):
+        need = {}
+
+        def want(rec):
+            sem, val, order = rec[2], rec[3], rec[4]
+            if clk[q].get(sem, 0) >= val:
+                return
+            if sem in DS:
+                val = cnt[sem]
+            if need.get(sem, (0, 0))[0] < val:
+                need[sem] = (val, order)
+        for r0 in ins:
+            r = bank(r0)
+            for rec in acc.get(r[0], []):
+                if hit(r, rec[0]) and (rec[1] or (r[0] == "ps" and rec[5] != q)):
+                    want(rec)
+        for r0 in outs:
+            r = bank(r0)
+            for rec in acc.get(r[0], []):
+                if hit(r, rec[0]) and not (rec[5] == q == "t"):
+                    want(rec)
+        for sem, (val, order) in sorted(need.items(), key=lambda e: -e[1][1]):
+            if clk[q].get(sem, 0) < val:
+                eng[q].wait_ge(T.sem[sem], val)
+                merge(q, sem, val)
+        made = call()
+        seq[0] += 1
+        if remote:
+            return
+        sem = dma or QS[q]
+        cnt[sem] = cnt.get(sem, 0) + (16 if dma else 1)
+        made.then_inc(T.sem[sem], 16 if dma else 1)
+        snaps.setdefault(sem, []).append((cnt[sem], dict(clk[q])))
+        for r0, wr in [(r, True) for r in outs] + [(r, False) for r in ins]:
+            r = bank(r0)
+            lst = acc.setdefault(r[0], [])
+            if wr:
+                lst[:] = [e for e in lst if not (e[0][1] >= r[1] and e[0][2] <= r[2] and e[0][3] >= r[3] and e[0][4] <= r[4] and r[5] == 1)]
+            lst.append((r, wr, sem, cnt[sem], seq[0], q, dma))
+
+    def arrive(regs, sem, val):
+        seq[0] += 1
+        for r in regs:
+            acc.setdefault(r[0], []).append((r, True, sem, val, seq[0], "r", sem))
+
+    def finish(extra):
+        for sem in list(cnt):
+            if clk["g"].get(sem, 0) < cnt[sem]:
+                g.wait_ge(T.sem[sem], cnt[sem])
+                merge("g", sem, cnt[sem])
+        for sem, val in extra:
+            if clk["g"].get(sem, 0) < val:
+                g.wait_ge(T.sem[sem], val)
+    return emit, arrive, finish
+
+
+def rank_program(g, core, T, topo):
+    rank = T.rank_of(core)
+    if rank is None:
+        return
+    N = len(T.cores)
+    nxt, prv = T.cores[(rank + 1) % N], T.cores[(rank - 1) % N]
+    A, AF = AluOpType, ActivationFunctionType
+    emit, arrive, finish = make_tracker(g, T)
+
+    def W(n, c0=0, c1=None, s=1, p0=0, p1=128):
+        return (n, p0, p1, c0, c1 if c1 is not None else (SCRATCH[n][1][1] if n in SCRATCH else T[n].shape[1]), s)
+
+    def ap(r):
+        if len(r) == 2:
+            return ap(r[0]).indirect(ap(r[1]))
+        n, p0, p1, c0, c1, s = r
+        return T[n][p0:p1, c0:c1] if s == 1 else T[n][p0:p1, c0:c1:s]
+
+    def by(r):
+        return ap(r).bitcast(dt.uint8)
+
+    def rg(*rs):
+        o = []
+        for r in rs:
+            o += list(r) if len(r) == 2 else [r]
+        return o
+
+    def ind(win, off):
+        return (win, off)
+
+    def tt(out, a, b, op):
+        emit("v", lambda: g.vector.tensor_tensor(ap(out), ap(a), ap(b), op), rg(out), rg(a, b))
+
+    def ts(out, a, s1, op0, s2=None, op1=None):
+        x1, x2 = (ap(s) if isinstance(s, tuple) else s for s in (s1, s2))
+        sc = [s for s in (s1, s2) if isinstance(s, tuple)]
+        if op1 is None:
+            emit("v", lambda: g.vector.tensor_scalar(ap(out), ap(a), x1, None, op0), rg(out), rg(a, *sc))
+        else:
+            emit("v", lambda: g.vector.tensor_scalar(ap(out), ap(a), x1, x2, op0, op1), rg(out), rg(a, *sc))
+
+    def cp(out, a):
+        emit("v", lambda: g.vector.tensor_copy(ap(out), ap(a)), rg(out), rg(a))
+
+    def scatter(win, off, a):
+        emit("v", lambda: g.vector.tensor_copy(ap((win, off)), ap(a)), [win], [off, a])
+
+    def fill(out, val):
+        emit("v", lambda: g.vector.memset(ap(out), val), rg(out), [])
+
+    def act(out, a, fn, scale=1.0, bias=0.0, accum=None):
+        kw = {}
+        if scale != 1.0:
+            kw["scale"] = scale
+        if bias != 0.0:
+            kw["bias"] = bias
+        if accum is not None:
+            kw["accum_out"] = ap(accum)
+        emit("a", lambda: g.scalar.activation(ap(out), ap(a), fn, **kw), rg(out, accum) if accum is not None else rg(out), rg(a))
+
+    def iota(out, pattern, base=0, cm=0):
+        kw = {} if SCRATCH[out[0]][2] == I32 else {"allow_small_or_imprecise_dtypes": True}
+        emit("g", lambda: g.iota(ap(out), pattern, base, cm, **kw), rg(out), [])
+
+    def asel(out, a, pattern, op, base, cm):
+        emit("g", lambda: g.affine_select(ap(out), ap(a), pattern, op, 0.0, base, cm), rg(out), rg(a))
+
+    def dma(q, sem, out, a, o8=False, a8=False):
+        e = {"s": g.sync, "a": g.scalar}[q]
+        emit(q, lambda: e.dma_start(by(out) if o8 else ap(out), by(a) if a8 else ap(a)), rg(out), rg(a), dma=sem)
+
+    def rows_on(q, sem, out, o0, o1, src, n, d):
+        for p0, p1, to in ((0, 128 - 16 * d, 16 * d), (128 - 16 * d, 128, 0)):
+            if p0 < p1:
+                o, a = W(out, o0, o1, p0=to, p1=to + p1 - p0), W(src, p0=p0, p1=p1)
+                e = {"s": g.sync, "a": g.scalar}[q]
+                emit(q, lambda: e.dma_start(ap(o), T[src][p0:p1:16, 0:n]), [o], [a], dma=sem)
+
+    def quant(n, c0, c1, src):
+        o, s = W(n, c0, c1), W(n + "s", c0, c1)
+        emit("v", lambda: g.vector.quantize_mx(ap(o), ap(s), ap(src)), rg(o, s), rg(src))
+
+    def mm(bank, wn, w0, xn, x0, n, start=True, stop=True):
+        o = W("ps", 512 * bank, 512 * bank + n)
+        w, ws, x, xs = W(wn, w0, w0 + 128), W(wn + "s", w0, w0 + 128), W(xn, x0, x0 + n), W(xn + "s", x0, x0 + n)
+        emit("t", lambda: g.tensor.matmul_mx(ap(o), ap(w), ap(ws), ap(x), ap(xs), start, stop), rg(o), rg(w, ws, x, xs))
+
+    def bk(b, c0, c1):
+        return W("ps", 512 * b + c0, 512 * b + c1)
+
+    def pick(out, src, off):
+        emit("v", lambda: g.vector.tensor_copy(ap(W(out)).bitcast(dt.uint32), ap(W(src)).bitcast(dt.uint32).indirect(ap(off))), rg(W(out)), rg(W(src), off))
+        emit("v", lambda: g.vector.tensor_copy(ap(W(out + "s")), ap(W(src + "s")).indirect(ap(off))), rg(W(out + "s")), rg(W(src + "s"), off))
+
+    LF, LH, LB, LHE = (W("pflt", i, i + 1) for i in range(4))
+    PI, LI, LHI, LBI = (W("pint", i, i + 1) for i in range(4))
+
+    dma("s", "du", W("ub"), W("u"))
+    dma("a", "dx", W("x0"), W("x"))
+    dma("a", "drv", W("rvt"), W("rv"))
+    dma("s", "dwc", W("wq"), W("wc"), o8=True)
+    dma("s", "dws", W("wqs"), W("ws"))
+    dma("s", "dv", W("vb"), W("v"))
+
+    C8, C1, C16, KC = W("cs", 0, 8), W("cs", 8, 8 + NJ), W("cs", 32, 32 + NJ), W("cs", 64, 64 + NJ)
+    iota(PI, [[0, 1]], 0, 1)
+    iota(C8, [[16, 8]])
+    iota(C16, [[16, NJ]])
+    iota(C1, [[1, NJ]])
+    iota(W("r16"), [[0, NJ], [1, 16]])
+    iota(W("ic"), [[1, C]])
+    iota(KC, [[-16, NJ]], C - 1)
+    fill(W("negb"), -1.0)
+    fill(W("onesb"), 1.0)
+    cp(W("sOM", 0, 8), C8)
+    ts(W("sOM", 8, 16), C8, 8.0, A.add)
+    asel(W("negb"), W("negb"), [[-16, 8], [0, 64]], A.is_ge, 0, 1)
+    asel(W("negb"), W("negb"), [[16, 8], [0, 64]], A.is_ge, 15, -1)
+    asel(W("cb", 4 * CC, 4 * CC + 512), W("negb"), [[0, 32], [1, 4], [-1, 4]], A.is_equal, 0, 0)
+    asel(W("cb", 4 * CT, 4 * CT + 512), W("cb", 4 * CC, 4 * CC + 512), [[1, 128], [0, 4]], A.is_ge, -1, -1)
+    iota(W("r4"), [[0, 72], [1, 4]])
+    for b in range(4):
+        asel(W("cb", 512 * b, 512 * b + 512), W("onesb"), [[-1, 512]], A.is_equal, b, 4)
+    iota(W("a32"), [[32, 28]], 4)
+    iota(W("dmy"), [[1, K]], C)
+    iota(W("r0c"), [[2, K]], 1)
+    fill(W("G", 288 * 9, 4 * GW), 0.0)
+    ts(LI, PI, 15, A.bitwise_and)
+    for s in range(1, 9):
+        fill(W("G", 288 * s + 288 - 16 * s, 288 * s + 288), 0.0)
+    cp(LF, LI)
+    cp(W("lOE"), C1)
+    ts(W("m16"), W("r16"), LF, A.is_equal)
+    quant("qu", 0, 128, W("ub"))
+    pick("uo", "qu", W("sOM", 0, 8))
+    pick("um", "qu", W("sOM", 8, 16))
+    ts(LHI, LI, 2, A.logical_shift_right)
+    ts(LBI, LI, 3, A.bitwise_and)
+
+    def consts_compare():
+        cp(LH, LHI)
+        cp(LB, LBI)
+        fill(W("Rs", 0, 1), 0.0)
+        fill(W("Bx", 0, 1), 0.0)
+        ts(W("yl"), C16, LF, A.add)
+        ts(W("lrv"), W("yl"), -1.0, A.mult, float(C - 1), A.add)
+
+    def consts_count():
+        quant("cq", CC, CZ, W("cb", 4 * CC, 4 * CZ))
+        quant("gq", 72 * 16, GW, W("G", 288 * 16, 4 * GW))
+
+    def consts_place():
+        ts(W("m4"), W("r4"), LH, A.is_equal)
+        cp(W("rvl"), W("rvt"))
+        ts(W("yo"), W("ic"), 1.0, A.subtract, 0.0, A.max)
+        ts(W("ya"), W("yl"), -8.5, A.add, 1.0 / 18, A.mult)
+        ts(W("yo"), W("yo"), -1.0 / UNIT, A.mult, (C - 1) / UNIT, A.add)
+        cp(W("yi"), W("ya"))
+        ts(W("ya"), W("yl"), 16.0, A.mult)
+        cp(W("T4"), ind(W("yo"), W("rvl")))
+        ts(W("yb"), W("yi"), -287.0, A.mult)
+        cp(W("wr"), ind(W("T4"), W("lrv")))
+        tt(W("yb"), W("yb"), W("ya"), A.add)
+        cp(W("lp18"), W("yb"))
+
+    def consts_odd():
+        ts(W("ya"), W("yl"), -3.0, A.add, 1.0 / 7, A.mult)
+        quant("cq", CE, CC, W("cb", 0, 4 * CC))
+        cp(W("yi"), W("ya"))
+        ts(W("ya"), W("yl"), 16.0, A.mult)
+        ts(W("yb"), W("yi"), -111.0, A.mult)
+        tt(W("yb"), W("yb"), W("ya"), A.add)
+        cp(W("lp7", 0, 7), W("yb", 0, 7))
+        ts(W("lpo", 0, 7), W("yb", 0, 7), 2.0, A.mult, 1.0, A.add)
+
+    def consts_cuts():
+        ts(LHE, LH, 8.0, A.mult)
+        ts(W("r0c"), W("r0c"), 1.0 / UNIT, A.mult)
+        ts(W("yc"), W("a32"), LHE, A.add)
+        ts(W("lrq", 0, 7), W("yl", 0, 7), -1.0, A.mult, float(K - 1), A.add)
+        ts(W("lA"), W("yc"), LB, A.add)
+        fill(W("kb", K - 1, K), 0.0)
+        fill(W("Et", 448, 512), 0.0)
+        fill(W("Vt", 448, 512), 0.0)
+        fill(W("pls"), 0)
+        fill(W("cb", 4 * CZ, 4 * CZ + 512), 0.0)
+        quant("cq", CZ, CZ + 128, W("cb", 4 * CZ, 4 * CZ + 512))
+
+    def pads():
+        for t in range(ROUNDS):
+            dma("s", "dz", W("le", 128 * t + K, 128 * t + 128), W("cq", CZ, CZ + 128 - K), o8=True, a8=True)
+            dma("s", "dz", W("les", 128 * t + K, 128 * t + 128), W("cqs", CZ, CZ + 128 - K))
+
+    def fold(src, n, levels):
+        for name in levels:
+            n //= 2
+            tt(W(name, 0, n), (src[0], 0, 128, 0, 2 * n, 2), (src[0], 0, 128, 1, 2 * n, 2), A.add)
+            src = W(name, 0, n)
+        return src
+
+    def to28(row, out, scale):
+        tt(W("w"), row, W("m4", 0, K), A.mult)
+        ts(out, fold(W("w"), K, ["w1", "w2"]), scale, A.mult, LB, A.add)
+
+    ne, np_ = len(topo.engines(core, nxt)[:8]), len(topo.engines(prv, core)[:8])
+    emask = sum(1 << e for e in topo.engines(core, nxt)[:8])
+    rid, pid = topo.addr(nxt, core)
+    rlc = [0]
+
+    def send(out_ap, src, in_ap, sem):
+        emit("g", lambda: g.remote_dma(out_ap, in_ap, T.sem[sem], T.sem.rl, pid, rid, emask), [], [src], remote=True)
+        rlc[0] += ne
+
+    for t in range(ROUNDS):
+        quant("qx", 0, C, W("x0") if t == 0 else W("X", 0, 4 * C))
+        mm(0, "uo", 0, "qx", 0, C)
+        mm(1, "um", 0, "qx", 0, C)
+        if t == 0:
+            consts_compare()
+        So = bk(0, 0, C)
+        tt(W("z"), So, W("m16"), A.mult)
+        act(W("sg"), bk(1, 0, C), AF.Sign)
+        fold(W("z"), C, ["z1", "z2", "z3", "own"])
+        act(W("sg2"), W("sg"), AF.Sign, bias=-0.5)
+        act(W("OE"), ind(W("own", 0, NJ), W("lOE")), AF.Copy)
+
+        def chunk(k, n):
+            quant("gq", 288 * k, 288 * k + 72 * n, W("G", 1152 * k, 1152 * k + 288 * n))
+            for s in range(max(4 * k - 1, 0), 4 * k + n - (n == 4)):
+                mm(6, "cq", CT if s == NJ else CC, "gq", 72 * s, 128, start=(s == 0), stop=(s == NJ))
+        for s in range(SLOTS):
+            if s % 4 == 1 and s > 1:
+                if t == 0 and s == 5:
+                    consts_count()
+                chunk(s // 4 - 1, 4)
+            if s < NJ:
+                j = NJ - 1 - s
+                ts(W("G", 288 * s, 288 * s + 16 * j + 16), bk(0, 0, 16 * j + 16), W("own", j, j + 1), A.is_lt)
+                if j:
+                    act(W("junk", 288 * (s % 4), 288 * (s % 4) + 16 * j), W("G", 288 * s, 288 * s + 16 * j), AF.Copy, accum=W("Rs", j, j + 1))
+            else:
+                tt(W("G", 288 * s, 288 * s + 288), So, W("OE"), A.is_equal)
+        chunk(4, 3)
+        if t == 0:
+            ts(W("I"), W("ic"), 1.0 / UNIT, A.mult)
+            consts_place()
+        tt(W("Vr"), W("sg2"), W("I"), A.add)
+        tt(W("R2"), W("Rs"), KC, A.add)
+        tt(W("z2"), bk(6, 0, 72), W("m4", 0, 72), A.mult)
+        tt(W("rk"), fold(W("z2"), 72, ["z3", "z1"]), W("R2"), A.add)
+        cp(W("rkl"), W("rk"))
+        scatter(W("PL"), W("rkl"), W("Vr"))
+        tt(W("am"), W("PL"), W("wr"), A.min)
+        emit("v", lambda: g.vector.tensor_tensor_scan(ap(W("Bx", 1, C + 1)), ap(W("am")), ap(W("am")), 0.0, A.max, A.max), [W("Bx", 1, C + 1)], [W("am")])
+        dma("s", "dT1", W("T1", p0=16), W("Bx", 0, C, p1=112))
+        dma("s", "dT1", W("T1", p1=16), W("Bx", 0, C, p0=112))
+        ts(W("Bp"), ind(W("Bx", 0, C), W("lp18")), UNIT, A.mult)
+        rows_on("s", "dL2", "L2", 0, NJ, "Bp", C, 2)
+        rows_on("s", "dL3", "L3", 0, NJ, "Bp", C, 3)
+        if t == 0:
+            consts_odd()
+        ts(W("Bo"), ind(W("Bx", 0, C), W("lpo", 0, 7)), UNIT, A.mult)
+        rows_on("s", "dLo", "Lo", 0, 7, "Bo", K, 4)
+        rows_on("s", "dL4", "L4", 0, NJ, "Bp", C, 4)
+        rows_on("s", "dL4", "L1", 0, NJ, "Bp", C, 1)
+        for b in range(4):
+            mm(2 + b, "cq", 128 * b, "qx", 0, C)
+        for b in range(4):
+            act(W("X", b, 4 * C, 4), bk(2 + b, 0, C), AF.Copy)
+        ts(W("oi1"), W("PL"), UNIT, A.mult, UNIT, A.add)
+        ts(W("oi"), W("oi1"), 1023, A.bitwise_and)
+        tt(W("z"), W("oi"), W("m4"), A.mult)
+        r = fold(W("z"), C, ["z1", "z2"])
+        ts(W("lo"), r, 4.0, A.mult, LB, A.add)
+        if t == 0:
+            consts_cuts()
+            pads()
+        act(W("FS"), ind(W("X", 0, 4 * C), W("lo")), AF.Copy, scale=2.0 ** -5)
+        act(W("A5"), ind(W("FS"), W("lA")), AF.Copy)
+        odd = [(n, 0, 128, 1, 2 * K, 2) for n in ("T1", "T2", "T3")]
+        tt(W("P1"), odd[0], W("r0c"), A.max)
+        cp(W("T2"), ind(W("T1"), W("L2")))
+        cp(W("T3"), ind(W("T2"), W("L3")))
+        tt(W("P2"), odd[1], W("P1"), A.max)
+        tt(W("P3"), odd[2], W("P2"), A.max)
+        tt(W("P4"), ind(W("T3"), W("Lo", 0, 7)), W("P3"), A.max)
+        ts(W("Pp"), ind(W("P4"), W("lp7", 0, 7)), UNIT, A.mult)
+        o = 40 * t
+        for d in range(5):
+            rows_on("sa"[d % 2], "dP", "pls", o + 8 * d, o + 8 * d + 7, "Pp", K, d)
+        to28(W("P4"), W("lE"), 4 * UNIT)
+        tt(W("Et", 0, 448), ind(W("FS"), W("lE")), W("A5"), A.add)
+        quant("eq", 128 * t, 128 * t + 128, W("Et"))
+        pl, plo = W("pls", o, o + 40), W("pll", o, o + 40)
+        e, eo = W("eq", 128 * t, 128 * t + K), W("le", 128 * t, 128 * t + K)
+        send(by(eo), e, by(e), "ae%d" % t)
+        send(ap(plo), pl, ap(pl), "ap%d" % t)
+        es, eso = W("eqs", 128 * t, 128 * t + K), W("les", 128 * t, 128 * t + K)
+        send(ap(eso), es, ap(es), "ae%d" % t)
+        ts(W("yo"), W("oi"), 1.0 / (TAGU * UNIT), A.mult)
+        tt(W("TAG"), W("yo"), W("I"), A.add)
+        act(W("Q1"), ind(W("TAG"), W("L1")), AF.Copy)
+        for d in (2, 3, 4):
+            act(W("Q%d" % d), ind(W("Q%d" % (d - 1)), W("L%d" % d)), AF.Copy)
+        arrive([plo], "ap%d" % t, np_)
+        arrive([eo, eso], "ae%d" % t, 2 * np_)
+        for b in range(4):
+            mm(2 + b, "cq", 128 * b, "le", 128 * t, 128)
+        for b in range(4):
+            act(W("DE", b, 448, 4), bk(2 + b, 0, K), AF.Copy, scale=0.5)
+        cp(W("q0"), ind(W("Q1"), W("pll", o + 8, o + 15)))
+        tt(W("q1"), ind(W("TAG"), W("pll", o, o + 7)), W("q0"), A.max)
+        tt(W("q0"), ind(W("Q2"), W("pll", o + 16, o + 23)), W("q1"), A.max)
+        tt(W("q1"), ind(W("Q3"), W("pll", o + 24, o + 31)), W("q0"), A.max)
+        tt(W("q4"), ind(W("Q4"), W("pll", o + 32, o + 39)), W("q1"), A.max)
+        to28(W("q4"), W("lQ"), 4 * UNIT)
+        tt(W("Vt", 0, 448), ind(W("FS"), W("lQ")), W("DE"), A.add)
+        act(W("FQ"), ind(W("FS"), W("lQ")), AF.Copy, scale=32.0)
+        quant("vq", 0, 128, W("Vt"))
+        hb = (0, 1, 6, 7)
+        for b in range(4):
+            mm(hb[b], "wq", 128 * b, "vq", 0, 128)
+        ts(W("qi"), W("q4"), TAGU * UNIT, A.mult)
+        tt(W("eqn", 0, K - 1), W("q4", 0, K - 1), W("q4", 1, K), A.is_equal)
+        ts(W("qj"), W("qi"), 511, A.bitwise_and)
+        tt(W("kb", 0, K - 1), W("eqn", 0, K - 1), W("dmy", 0, K - 1), A.mult)
+        tt(W("sel"), W("qj"), W("kb"), A.max)
+        tt(W("CV", 0, 448, 4), bk(hb[0], 0, K), W("FQ", 0, 448, 4), A.add)
+        tt(W("w"), W("sel"), W("m4", 0, K), A.mult)
+        tt(W("CV", 1, 448, 4), bk(hb[1], 0, K), W("FQ", 1, 448, 4), A.add)
+        fold(W("w"), K, ["w1"])
+        tt(W("CV", 2, 448, 4), bk(hb[2], 0, K), W("FQ", 2, 448, 4), A.add)
+        r = fold(W("w1"), 56, ["w2"])
+        tt(W("CV", 3, 448, 4), bk(hb[3], 0, K), W("FQ", 3, 448, 4), A.add)
+        ts(W("lX"), r, 4.0, A.mult, LB, A.add)
+        scatter(W("X"), W("lX"), W("CV"))
+        if t == 0:
+            quant("qv", 0, 128, W("vb"))
+    quant("qx", 0, C, W("X", 0, 4 * C))
+    mm(0, "qv", 0, "qx", 0, C)
+    emit("s", lambda: g.sync.dma_start(T.oc[:, :], by(W("qx"))), [], [W("qx")], dma="doc")
+    ts(W("qj"), ind(W("q4"), W("lrq", 0, 7)), UNIT, A.mult)
+    act(W("yo"), bk(0, 0, C), AF.Copy)
+    ts(W("lqf"), W("qj"), -1.0, A.mult, float(C - 1), A.add)
+    emit("a", lambda: g.scalar.dma_start(T.y[:, :], T.yo[:, :]), [], [W("yo")], dma="dy")
+    for k in range(4):
+        emit("s", lambda: g.sync.dma_start(T.osc[4 * k:4 * k + 4, :], T.qxs[32 * k:32 * k + 4, 0:C]), [], [W("qxs")], dma="doc")
+    emit("s", lambda: g.sync.dma_start(T.lq[:, :], T.lqf[0:128:16, 0:K]), [], [W("lqf")], dma="dlq")
+    finish([("rl", rlc[0])] + [("ap%d" % t, np_) for t in range(ROUNDS)] + [("ae%d" % t, 2 * np_) for t in range(ROUNDS)])

@@ -5,6 +5,7 @@ NJ = C // 16
 UNIT = 1024.0
 TAGU = 4096.0
 CODE, F32, BF, I32, U16, U8 = "float8_e4m3fn_x4", "float32", "bfloat16", "int32", "uint16", "uint8"
+SB = (9, 8, 7)
 SLOTS = NJ + 1
 GW = 72 * SLOTS + 72
 CE, CC, CT, CZ = 0, 512, 640, 768
@@ -17,16 +18,16 @@ def _sb(dtype, **names):
         SCRATCH[n] = ("sbuf", [128, w], dtype)
 
 
-_sb(BF, x0=4 * C, X=1600, ub=512, vb=512, onesb=512, negb=512, cb=4 * 896, G=4 * GW, m4=C, m16=C, junk=4 * C,
+_sb(BF, x0=4 * C, X=1600, ub=512, vb=512, nega=512, negb=512, cb=4 * 768, G=4 * GW, m4=C, m16=C, junk=4 * C,
     FS=4 * C, A5=448, Et=512, Vt=512, DE=448, CV=448)
-_sb(F32, r4=C, r16=C, pflt=4, ic=C, I=C, r0c=K, dmy=K, cs=96, yl=NJ, ya=NJ, yb=NJ, yc=28, yd=28, a32=28, wr=C,
-    z=C, z1=144, z2=72, z3=36, own=24, OE=C, sg=C, sg2=C, Vr=C, Rs=NJ, R2=NJ, rk=NJ, PL=C, am=C, Bx=292, TAG=C,
-    T1=C, T2=C, T3=C, T4=C, Q1=C, Q2=C, Q3=C, Q4=C, P1=K, P2=K, P3=K, P4=K, w=K, w1=56, w2=28, FQ=448, eqn=K, kb=K, sel=K, lqf=K,
+_sb(F32, r4=C, r16=C, pflt=8, ic=C, I=C, dmy=K, cs=96, yl=NJ, ya=NJ, yb=NJ, yc=28, yd=28, wr=C,
+    z=C, zs=C, zz=144, KK=2 * C, M1=K, OE=C, sg=C, Vr=C, Rs=NJ, R2=NJ, rk=NJ, PL=C, am=C, rl=480, Bx=292, TAG=C,
+    T1=C, T2=C, T3=C, T4=C, Q1=C, Q2=C, Q3=C, Q4=C, P1=K, P2=K, P3=K, P4=K, w=K, w1=K, wE=K, FQ=448, eqn=K, sel=28, lqf=K,
     q0=K, q1=K, q4=K, yo=C)
-_sb(I32, rvt=NJ, pint=4, yi=NJ, oi1=C, oi=C, qi=K, qj=K)
+_sb(I32, rvt=NJ, pint=8, yi=NJ, yj=NJ, oi1=C, oi=C, qi=28, qj=28, qz=K)
 _sb(U16, rvl=NJ, sOM=16, lOE=NJ, lp18=NJ, lp7=8, lpo=8, Bo=K, Lo=8, lrv=NJ, lrq=8, lA=28, rkl=NJ, Bp=C, L1=NJ, L2=NJ, L3=NJ, L4=NJ, lo=72,
     Pp=K, lE=28, lQ=28, lX=28, pls=40 * ROUNDS, pll=40 * ROUNDS)
-for _n, _w in [("qx", C), ("qu", 128), ("qv", 128), ("uo", 128), ("um", 128), ("wq", 512), ("cq", 896), ("gq", GW), ("vq", 128),
+for _n, _w in [("qx", C), ("qu", 128), ("qv", 128), ("uo", 128), ("um", 128), ("wq", 512), ("cq", 768), ("gq", GW), ("vq", 128),
                ("eq", 128 * ROUNDS), ("le", 128 * ROUNDS)]:
     SCRATCH[_n] = ("sbuf", [128, _w], CODE)
     SCRATCH[_n + "s"] = ("sbuf", [128, _w], U8)
@@ -42,7 +43,7 @@ def make_tracker(g, T):
     cnt = {}
     snaps = {}
     acc = {}
-    seq, cur = [0], [None]
+    seq = [0]
 
     def hit(a, b):
         if a[1] >= b[2] or b[1] >= a[2] or a[3] >= b[4] or b[3] >= a[4]:
@@ -166,15 +167,22 @@ def rank_program(g, core, T, topo):
     def fill(out, val):
         emit("v", lambda: g.vector.memset(ap(out), val), rg(out), [])
 
+    def scan(out, d0, d1, init, op0, op1):
+        emit("v", lambda: g.vector.tensor_tensor_scan(ap(out), ap(d0), ap(d1), init, op0, op1), [out], [d0, d1])
+
     def act(out, a, fn, scale=1.0, bias=0.0, accum=None):
-        kw = {}
+        kw, ins, outs = {}, rg(a), rg(out)
         if scale != 1.0:
             kw["scale"] = scale
-        if bias != 0.0:
+        if isinstance(bias, tuple):
+            kw["bias"] = ap(bias)
+            ins.append(bias)
+        elif bias != 0.0:
             kw["bias"] = bias
         if accum is not None:
             kw["accum_out"] = ap(accum)
-        emit("a", lambda: g.scalar.activation(ap(out), ap(a), fn, **kw), rg(out, accum) if accum is not None else rg(out), rg(a))
+            outs.append(accum)
+        emit("a", lambda: g.scalar.activation(ap(out), ap(a), fn, **kw), outs, ins)
 
     def iota(out, pattern, base=0, cm=0):
         kw = {} if SCRATCH[out[0]][2] == I32 else {"allow_small_or_imprecise_dtypes": True}
@@ -206,12 +214,21 @@ def rank_program(g, core, T, topo):
     def bk(b, c0, c1):
         return W("ps", 512 * b + c0, 512 * b + c1)
 
-    def pick(out, src, off):
-        emit("v", lambda: g.vector.tensor_copy(ap(W(out)).bitcast(dt.uint32), ap(W(src)).bitcast(dt.uint32).indirect(ap(off))), rg(W(out)), rg(W(src), off))
-        emit("v", lambda: g.vector.tensor_copy(ap(W(out + "s")), ap(W(src + "s")).indirect(ap(off))), rg(W(out + "s")), rg(W(src + "s"), off))
+    def pick(out, off):
+        emit("v", lambda: g.vector.tensor_copy(ap(W(out)).bitcast(dt.uint32), ap(W("qu")).bitcast(dt.uint32).indirect(ap(off))), [W(out)], [W("qu"), off])
+        emit("a", lambda: g.scalar.activation(ap(W(out + "s")), ap(W("qus")).indirect(ap(off)), AF.Copy), [W(out + "s")], [W("qus"), off])
 
-    LF, LH, LB, LHE = (W("pflt", i, i + 1) for i in range(4))
-    PI, LI, LHI, LBI = (W("pint", i, i + 1) for i in range(4))
+    LF, LH, LB, LHE, LP, LZ, LBZ = (W("pflt", i, i + 1) for i in range(7))
+    PI, LI, LHI, LBI, LPI, LPJ = (W("pint", i, i + 1) for i in range(6))
+    C8, C28, C16, KC = W("cs", 0, 8), W("cs", 32, 60), W("cs", 32, 32 + NJ), W("cs", 64, 64 + NJ)
+    B16, B4 = W("KK", 0, C), W("KK", C, 2 * C)
+
+    def last(out, a, keep):
+        scan(out, keep, a, 0.0, A.mult, A.add)
+
+    def to28(row, tmp, out):
+        scan(tmp, row, W("M1"), 1.0, A.min, A.add)
+        ts(out, (tmp[0], 0, 128, 3, K, 4), 4 * UNIT, A.mult, LBZ, A.add)
 
     dma("s", "du", W("ub"), W("u"))
     dma("a", "dx", W("x0"), W("x"))
@@ -220,105 +237,86 @@ def rank_program(g, core, T, topo):
     dma("s", "dws", W("wqs"), W("ws"))
     dma("s", "dv", W("vb"), W("v"))
 
-    C8, C1, C16, KC = W("cs", 0, 8), W("cs", 8, 8 + NJ), W("cs", 32, 32 + NJ), W("cs", 64, 64 + NJ)
     iota(PI, [[0, 1]], 0, 1)
     iota(C8, [[16, 8]])
-    iota(C16, [[16, NJ]])
-    iota(C1, [[1, NJ]])
-    iota(W("r16"), [[0, NJ], [1, 16]])
     iota(W("ic"), [[1, C]])
+    iota(C28, [[16, 28]])
+    iota(W("r16"), [[0, NJ], [1, 16]])
+    iota(W("r4"), [[0, 72], [1, 4]])
     iota(KC, [[-16, NJ]], C - 1)
-    fill(W("negb"), -1.0)
-    fill(W("onesb"), 1.0)
+    fill(W("nega"), -1.0)
+    ts(LI, PI, 15, A.bitwise_and)
     cp(W("sOM", 0, 8), C8)
     ts(W("sOM", 8, 16), C8, 8.0, A.add)
-    asel(W("negb"), W("negb"), [[-16, 8], [0, 64]], A.is_ge, 0, 1)
+    cp(LF, LI)
+    ts(LHI, LI, 2, A.logical_shift_right)
+    ts(LBI, LI, 3, A.bitwise_and)
+    for s in range(1, 9):
+        fill(W("G", 288 * s + 288 - 16 * s, 288 * s + 288), 0.0)
+    asel(W("negb"), W("nega"), [[-16, 8], [0, 64]], A.is_ge, 0, 1)
     asel(W("negb"), W("negb"), [[16, 8], [0, 64]], A.is_ge, 15, -1)
     asel(W("cb", 4 * CC, 4 * CC + 512), W("negb"), [[0, 32], [1, 4], [-1, 4]], A.is_equal, 0, 0)
     asel(W("cb", 4 * CT, 4 * CT + 512), W("cb", 4 * CC, 4 * CC + 512), [[1, 128], [0, 4]], A.is_ge, -1, -1)
-    iota(W("r4"), [[0, 72], [1, 4]])
     for b in range(4):
-        asel(W("cb", 512 * b, 512 * b + 512), W("onesb"), [[-1, 512]], A.is_equal, b, 4)
-    iota(W("a32"), [[32, 28]], 4)
-    iota(W("dmy"), [[1, K]], C)
-    iota(W("r0c"), [[2, K]], 1)
-    fill(W("G", 288 * 9, 4 * GW), 0.0)
-    ts(LI, PI, 15, A.bitwise_and)
-    for s in range(1, 9):
-        fill(W("G", 288 * s + 288 - 16 * s, 288 * s + 288), 0.0)
-    cp(LF, LI)
-    cp(W("lOE"), C1)
+        asel(W("cb", 512 * b, 512 * b + 512), W("nega"), [[-1, 512]], A.is_equal, b, 4)
+    for n in ("Et", "Vt"):
+        asel(W(n, 448, 512), W("nega", 0, 64), [[0, 64]], A.is_ge, -1, 0)
+    iota(W("w", K - 1, K), [[0, 1]])
+    cp(LH, LHI)
+    cp(LB, LBI)
+    ts(LPI, PI, 3.0 * 4, A.add)
+    ts(W("yl"), C16, LF, A.add)
+    ts(W("lOE"), C16, 15.0, A.add)
+    ts(LPJ, LPI, 2, A.logical_shift_right)
+    ts(W("ya"), W("yl"), -8.5, A.add, 1.0 / 18, A.mult)
+    ts(W("yd", 0, NJ), W("yl"), -3.0, A.add, 1.0 / 7, A.mult)
+    ts(LPI, LPJ, 3, A.bitwise_and)
+    cp(W("yi"), W("ya"))
+    cp(W("yj"), W("yd", 0, NJ))
+    ts(W("ya"), W("yl"), 16.0, A.mult)
     ts(W("m16"), W("r16"), LF, A.is_equal)
+    fill(W("pls"), 0)
+    cp(W("rvl"), W("rvt"))
+    act(W("yo"), W("ic"), AF.Relu, bias=-1.0)
+    act(W("I"), W("ic"), AF.Copy, scale=1.0 / UNIT)
+    act(W("T3"), W("yo"), AF.Identity, scale=-1.0 / UNIT, bias=(C - 1) / UNIT)
+    act(B16, W("r16"), AF.Sign)
+    act(B4, W("r4"), AF.Sign)
     quant("qu", 0, 128, W("ub"))
-    pick("uo", "qu", W("sOM", 0, 8))
-    pick("um", "qu", W("sOM", 8, 16))
-    ts(LHI, LI, 2, A.logical_shift_right)
-    ts(LBI, LI, 3, A.bitwise_and)
+    pick("uo", W("sOM", 0, 8))
 
-    def consts_compare():
-        cp(LH, LHI)
-        cp(LB, LBI)
-        fill(W("Rs", 0, 1), 0.0)
-        fill(W("Bx", 0, 1), 0.0)
-        ts(W("yl"), C16, LF, A.add)
-        ts(W("lrv"), W("yl"), -1.0, A.mult, float(C - 1), A.add)
+    def consts_first():
+        pick("um", W("sOM", 8, 16))
+        ts(W("m4"), W("r4"), LH, A.is_equal)
+        for s in list(range(9, NJ)) + [SLOTS]:
+            act(W("G", 288 * s, 288 * s + 288), W("ic"), AF.Copy, scale=0.0)
 
     def consts_count():
-        quant("cq", CC, CZ, W("cb", 4 * CC, 4 * CZ))
-        quant("gq", 72 * 16, GW, W("G", 288 * 16, 4 * GW))
-
-    def consts_place():
-        ts(W("m4"), W("r4"), LH, A.is_equal)
-        cp(W("rvl"), W("rvt"))
-        ts(W("yo"), W("ic"), 1.0, A.subtract, 0.0, A.max)
-        ts(W("ya"), W("yl"), -8.5, A.add, 1.0 / 18, A.mult)
-        ts(W("yo"), W("yo"), -1.0 / UNIT, A.mult, (C - 1) / UNIT, A.add)
-        cp(W("yi"), W("ya"))
-        ts(W("ya"), W("yl"), 16.0, A.mult)
-        cp(W("T4"), ind(W("yo"), W("rvl")))
         ts(W("yb"), W("yi"), -287.0, A.mult)
-        cp(W("wr"), ind(W("T4"), W("lrv")))
-        tt(W("yb"), W("yb"), W("ya"), A.add)
-        cp(W("lp18"), W("yb"))
-
-    def consts_odd():
-        ts(W("ya"), W("yl"), -3.0, A.add, 1.0 / 7, A.mult)
-        quant("cq", CE, CC, W("cb", 0, 4 * CC))
-        cp(W("yi"), W("ya"))
-        ts(W("ya"), W("yl"), 16.0, A.mult)
-        ts(W("yb"), W("yi"), -111.0, A.mult)
-        tt(W("yb"), W("yb"), W("ya"), A.add)
-        cp(W("lp7", 0, 7), W("yb", 0, 7))
-        ts(W("lpo", 0, 7), W("yb", 0, 7), 2.0, A.mult, 1.0, A.add)
-
-    def consts_cuts():
+        ts(W("yd", 0, NJ), W("yj"), -111.0, A.mult)
+        ts(W("lrv"), W("yl"), -1.0, A.mult, float(C - 1), A.add)
         ts(LHE, LH, 8.0, A.mult)
-        ts(W("r0c"), W("r0c"), 1.0 / UNIT, A.mult)
-        ts(W("yc"), W("a32"), LHE, A.add)
+        cp(LP, LPI)
+        ts(LZ, LH, 0.0, A.is_equal, -4.0 * UNIT, A.mult)
+        ts(W("yc"), C28, 2.0, A.mult, 4.0, A.add)
         ts(W("lrq", 0, 7), W("yl", 0, 7), -1.0, A.mult, float(K - 1), A.add)
+        ts(W("M1"), W("r4", 0, K), LP, A.is_equal)
+        tt(LBZ, LZ, LB, A.add)
+        ts(W("yc"), W("yc"), LHE, A.add)
         ts(W("lA"), W("yc"), LB, A.add)
-        fill(W("kb", K - 1, K), 0.0)
-        fill(W("Et", 448, 512), 0.0)
-        fill(W("Vt", 448, 512), 0.0)
-        fill(W("pls"), 0)
-        fill(W("cb", 4 * CZ, 4 * CZ + 512), 0.0)
-        quant("cq", CZ, CZ + 128, W("cb", 4 * CZ, 4 * CZ + 512))
+        quant("cq", CC, CZ, W("cb", 4 * CC, 4 * CZ))
+        tt(W("yb"), W("yb"), W("ya"), A.add)
+        tt(W("yd", 0, NJ), W("yd", 0, NJ), W("ya"), A.add)
+        fill(W("Rs", 0, 1), 0.0)
+        cp(W("lp18"), W("yb"))
+        cp(W("lp7", 0, 7), W("yd", 0, 7))
+        ts(W("lpo", 0, 7), W("yd", 0, 7), 2.0, A.mult, 1.0, A.add)
+        fill(W("Bx", 0, 1), 0.0)
 
     def pads():
         for t in range(ROUNDS):
-            dma("s", "dz", W("le", 128 * t + K, 128 * t + 128), W("cq", CZ, CZ + 128 - K), o8=True, a8=True)
-            dma("s", "dz", W("les", 128 * t + K, 128 * t + 128), W("cqs", CZ, CZ + 128 - K))
-
-    def fold(src, n, levels):
-        for name in levels:
-            n //= 2
-            tt(W(name, 0, n), (src[0], 0, 128, 0, 2 * n, 2), (src[0], 0, 128, 1, 2 * n, 2), A.add)
-            src = W(name, 0, n)
-        return src
-
-    def to28(row, out, scale):
-        tt(W("w"), row, W("m4", 0, K), A.mult)
-        ts(out, fold(W("w"), K, ["w1", "w2"]), scale, A.mult, LB, A.add)
+            dma("s", "dz", W("le", 128 * t + K, 128 * t + 128), W("eq", K, 128), o8=True, a8=True)
+            dma("s", "dz", W("les", 128 * t + K, 128 * t + 128), W("eqs", K, 128))
 
     ne, np_ = len(topo.engines(core, nxt)[:8]), len(topo.engines(prv, core)[:8])
     emask = sum(1 << e for e in topo.engines(core, nxt)[:8])
@@ -331,19 +329,28 @@ def rank_program(g, core, T, topo):
 
     for t in range(ROUNDS):
         quant("qx", 0, C, W("x0") if t == 0 else W("X", 0, 4 * C))
+        if t == 0:
+            consts_first()
         mm(0, "uo", 0, "qx", 0, C)
         mm(1, "um", 0, "qx", 0, C)
-        if t == 0:
-            consts_compare()
+        mm(7, "uo", 0, "qx", 0, C)
         So = bk(0, 0, C)
         tt(W("z"), So, W("m16"), A.mult)
         act(W("sg"), bk(1, 0, C), AF.Sign)
-        fold(W("z"), C, ["z1", "z2", "z3", "own"])
-        act(W("sg2"), W("sg"), AF.Sign, bias=-0.5)
-        act(W("OE"), ind(W("own", 0, NJ), W("lOE")), AF.Copy)
+        last(W("zs"), W("z"), B16)
+        act(W("sg"), W("sg"), AF.Sign, bias=-0.5)
+        for j in SB:
+            r = 160 * (j - SB[-1])
+            act(W("rl", r, r + 16 * j + 16), bk(7, 0, 16 * j + 16), AF.Relu, scale=-1.0, bias=W("zs", 16 * j + 15, 16 * j + 16))
+        for j in SB:
+            s, r = 288 * (NJ - 1 - j), 160 * (j - SB[-1])
+            act(W("G", s, s + 16 * j), W("rl", r, r + 16 * j), AF.Sign, accum=W("Rs", j, j + 1))
+            act(W("G", s + 16 * j, s + 16 * j + 16), W("rl", r + 16 * j, r + 16 * j + 16), AF.Sign)
+        act(W("OE"), ind(W("zs"), W("lOE")), AF.Copy)
 
         def chunk(k, n):
             quant("gq", 288 * k, 288 * k + 72 * n, W("G", 1152 * k, 1152 * k + 288 * n))
+            n = min(n, SLOTS - 4 * k)
             for s in range(max(4 * k - 1, 0), 4 * k + n - (n == 4)):
                 mm(6, "cq", CT if s == NJ else CC, "gq", 72 * s, 128, start=(s == 0), stop=(s == NJ))
         for s in range(SLOTS):
@@ -351,52 +358,50 @@ def rank_program(g, core, T, topo):
                 if t == 0 and s == 5:
                     consts_count()
                 chunk(s // 4 - 1, 4)
-            if s < NJ:
-                j = NJ - 1 - s
-                ts(W("G", 288 * s, 288 * s + 16 * j + 16), bk(0, 0, 16 * j + 16), W("own", j, j + 1), A.is_lt)
+            j = NJ - 1 - s
+            if j < 0:
+                tt(W("G", 288 * s, 288 * s + 288), So, W("OE"), A.is_equal)
+            elif j not in SB:
+                ts(W("G", 288 * s, 288 * s + 16 * j + 16), bk(0, 0, 16 * j + 16), W("zs", 16 * j + 15, 16 * j + 16), A.is_lt)
                 if j:
                     act(W("junk", 288 * (s % 4), 288 * (s % 4) + 16 * j), W("G", 288 * s, 288 * s + 16 * j), AF.Copy, accum=W("Rs", j, j + 1))
-            else:
-                tt(W("G", 288 * s, 288 * s + 288), So, W("OE"), A.is_equal)
-        chunk(4, 3)
+        chunk(4, 4 if t == 0 else 3)
         if t == 0:
-            ts(W("I"), W("ic"), 1.0 / UNIT, A.mult)
-            consts_place()
-        tt(W("Vr"), W("sg2"), W("I"), A.add)
+            act(W("T4"), ind(W("T3"), W("rvl")), AF.Copy)
+            act(W("wr"), ind(W("T4"), W("lrv")), AF.Copy)
+        tt(W("Vr"), W("sg"), W("I"), A.add)
+        tt(W("zz", 0, 72), bk(6, 0, 72), W("m4", 0, 72), A.mult)
+        last(W("zz", 72, 144), W("zz", 0, 72), W("KK", C, C + 72))
         tt(W("R2"), W("Rs"), KC, A.add)
-        tt(W("z2"), bk(6, 0, 72), W("m4", 0, 72), A.mult)
-        tt(W("rk"), fold(W("z2"), 72, ["z3", "z1"]), W("R2"), A.add)
+        tt(W("rk"), W("zz", 75, 144, 4), W("R2"), A.add)
         cp(W("rkl"), W("rk"))
         scatter(W("PL"), W("rkl"), W("Vr"))
         tt(W("am"), W("PL"), W("wr"), A.min)
-        emit("v", lambda: g.vector.tensor_tensor_scan(ap(W("Bx", 1, C + 1)), ap(W("am")), ap(W("am")), 0.0, A.max, A.max), [W("Bx", 1, C + 1)], [W("am")])
+        scan(W("Bx", 1, C + 1), W("am"), W("am"), 0.0, A.max, A.max)
         dma("s", "dT1", W("T1", p0=16), W("Bx", 0, C, p1=112))
         dma("s", "dT1", W("T1", p1=16), W("Bx", 0, C, p0=112))
         ts(W("Bp"), ind(W("Bx", 0, C), W("lp18")), UNIT, A.mult)
         rows_on("s", "dL2", "L2", 0, NJ, "Bp", C, 2)
         rows_on("s", "dL3", "L3", 0, NJ, "Bp", C, 3)
-        if t == 0:
-            consts_odd()
         ts(W("Bo"), ind(W("Bx", 0, C), W("lpo", 0, 7)), UNIT, A.mult)
         rows_on("s", "dLo", "Lo", 0, 7, "Bo", K, 4)
         rows_on("s", "dL4", "L4", 0, NJ, "Bp", C, 4)
         rows_on("s", "dL4", "L1", 0, NJ, "Bp", C, 1)
+        if t == 0:
+            quant("cq", CE, CC, W("cb", 0, 4 * CC))
         for b in range(4):
             mm(2 + b, "cq", 128 * b, "qx", 0, C)
         for b in range(4):
-            act(W("X", b, 4 * C, 4), bk(2 + b, 0, C), AF.Copy)
+            act(W("X", b, 4 * C, 4), bk(2 + b, 0, C), AF.Copy, scale=-1.0)
         ts(W("oi1"), W("PL"), UNIT, A.mult, UNIT, A.add)
         ts(W("oi"), W("oi1"), 1023, A.bitwise_and)
         tt(W("z"), W("oi"), W("m4"), A.mult)
-        r = fold(W("z"), C, ["z1", "z2"])
-        ts(W("lo"), r, 4.0, A.mult, LB, A.add)
-        if t == 0:
-            consts_cuts()
-            pads()
+        last(W("zs"), W("z"), B4)
+        ts(W("lo"), W("zs", 3, C, 4), 4.0, A.mult, LB, A.add)
         act(W("FS"), ind(W("X", 0, 4 * C), W("lo")), AF.Copy, scale=2.0 ** -5)
         act(W("A5"), ind(W("FS"), W("lA")), AF.Copy)
         odd = [(n, 0, 128, 1, 2 * K, 2) for n in ("T1", "T2", "T3")]
-        tt(W("P1"), odd[0], W("r0c"), A.max)
+        tt(W("P1"), odd[0], W("I", 1, 2 * K, 2), A.max)
         cp(W("T2"), ind(W("T1"), W("L2")))
         cp(W("T3"), ind(W("T2"), W("L3")))
         tt(W("P2"), odd[1], W("P1"), A.max)
@@ -406,15 +411,20 @@ def rank_program(g, core, T, topo):
         o = 40 * t
         for d in range(5):
             rows_on("sa"[d % 2], "dP", "pls", o + 8 * d, o + 8 * d + 7, "Pp", K, d)
-        to28(W("P4"), W("lE"), 4 * UNIT)
+        to28(W("P4"), W("wE"), W("lE"))
         tt(W("Et", 0, 448), ind(W("FS"), W("lE")), W("A5"), A.add)
         quant("eq", 128 * t, 128 * t + 128, W("Et"))
+        if t == 0:
+            pads()
         pl, plo = W("pls", o, o + 40), W("pll", o, o + 40)
         e, eo = W("eq", 128 * t, 128 * t + K), W("le", 128 * t, 128 * t + K)
         send(by(eo), e, by(e), "ae%d" % t)
         send(ap(plo), pl, ap(pl), "ap%d" % t)
         es, eso = W("eqs", 128 * t, 128 * t + K), W("les", 128 * t, 128 * t + K)
         send(ap(eso), es, ap(es), "ae%d" % t)
+        if t == 0:
+            act(W("T3", 0, K), W("ic", 0, K), AF.Identity, bias=float(C))
+            tt(W("dmy"), W("T3", 0, K), W("m4", 0, K), A.mult)
         ts(W("yo"), W("oi"), 1.0 / (TAGU * UNIT), A.mult)
         tt(W("TAG"), W("yo"), W("I"), A.add)
         act(W("Q1"), ind(W("TAG"), W("L1")), AF.Copy)
@@ -425,41 +435,38 @@ def rank_program(g, core, T, topo):
         for b in range(4):
             mm(2 + b, "cq", 128 * b, "le", 128 * t, 128)
         for b in range(4):
-            act(W("DE", b, 448, 4), bk(2 + b, 0, K), AF.Copy, scale=0.5)
+            act(W("DE", b, 448, 4), bk(2 + b, 0, K), AF.Copy, scale=-0.5)
         cp(W("q0"), ind(W("Q1"), W("pll", o + 8, o + 15)))
         tt(W("q1"), ind(W("TAG"), W("pll", o, o + 7)), W("q0"), A.max)
         tt(W("q0"), ind(W("Q2"), W("pll", o + 16, o + 23)), W("q1"), A.max)
         tt(W("q1"), ind(W("Q3"), W("pll", o + 24, o + 31)), W("q0"), A.max)
         tt(W("q4"), ind(W("Q4"), W("pll", o + 32, o + 39)), W("q1"), A.max)
-        to28(W("q4"), W("lQ"), 4 * UNIT)
+        to28(W("q4"), W("wE"), W("lQ"))
         tt(W("Vt", 0, 448), ind(W("FS"), W("lQ")), W("DE"), A.add)
         act(W("FQ"), ind(W("FS"), W("lQ")), AF.Copy, scale=32.0)
         quant("vq", 0, 128, W("Vt"))
         hb = (0, 1, 6, 7)
         for b in range(4):
             mm(hb[b], "wq", 128 * b, "vq", 0, 128)
-        ts(W("qi"), W("q4"), TAGU * UNIT, A.mult)
         tt(W("eqn", 0, K - 1), W("q4", 0, K - 1), W("q4", 1, K), A.is_equal)
+        ts(W("qi"), W("wE", 3, K, 4), TAGU * UNIT, A.mult)
+        tt(W("w", 0, K - 1), W("eqn", 0, K - 1), W("dmy", 0, K - 1), A.mult)
         ts(W("qj"), W("qi"), 511, A.bitwise_and)
-        tt(W("kb", 0, K - 1), W("eqn", 0, K - 1), W("dmy", 0, K - 1), A.mult)
-        tt(W("sel"), W("qj"), W("kb"), A.max)
-        tt(W("CV", 0, 448, 4), bk(hb[0], 0, K), W("FQ", 0, 448, 4), A.add)
-        tt(W("w"), W("sel"), W("m4", 0, K), A.mult)
-        tt(W("CV", 1, 448, 4), bk(hb[1], 0, K), W("FQ", 1, 448, 4), A.add)
-        fold(W("w"), K, ["w1"])
-        tt(W("CV", 2, 448, 4), bk(hb[2], 0, K), W("FQ", 2, 448, 4), A.add)
-        r = fold(W("w1"), 56, ["w2"])
+        last(W("w1"), W("w"), W("KK", C, C + K))
+        for b in range(3):
+            tt(W("CV", b, 448, 4), bk(hb[b], 0, K), W("FQ", b, 448, 4), A.add)
+        tt(W("sel"), W("qj"), W("w1", 3, K, 4), A.max)
         tt(W("CV", 3, 448, 4), bk(hb[3], 0, K), W("FQ", 3, 448, 4), A.add)
-        ts(W("lX"), r, 4.0, A.mult, LB, A.add)
+        ts(W("lX"), W("sel"), 4.0, A.mult, LB, A.add)
         scatter(W("X"), W("lX"), W("CV"))
         if t == 0:
             quant("qv", 0, 128, W("vb"))
     quant("qx", 0, C, W("X", 0, 4 * C))
     mm(0, "qv", 0, "qx", 0, C)
     emit("s", lambda: g.sync.dma_start(T.oc[:, :], by(W("qx"))), [], [W("qx")], dma="doc")
-    ts(W("qj"), ind(W("q4"), W("lrq", 0, 7)), UNIT, A.mult)
+    ts(W("qz"), ind(W("q4"), W("lrq", 0, 7)), UNIT, A.mult)
     act(W("yo"), bk(0, 0, C), AF.Copy)
-    ts(W("lqf"), W("qj"), -1.0, A.mult, float(C - 1), A.add)
+    ts(W("lqf"), W("qz"), -1.0, A.mult, float(C - 1), A.add)
     emit("a", lambda: g.scalar.dma_start(T.y[:, :], T.yo[:, :]), [], [W("yo")], dma="dy")
     for k in range(4):
         emit("s", lambda: g.sync.dma_start(T.osc[4 * k:4 * k + 4, :], T.qxs[32 * k:32 * k + 4, 0:C]), [], [W("qxs")], dma="doc")

from concourse.mybir import dt, AluOpType, ActivationFunctionType

C, K, ROUNDS = 288, 112, 3
NJ = C // 16
UNIT = 1024.0
TAGU = 4096.0
CODE, F32, BF, I32, U16, U8 = "float8_e4m3fn_x4", "float32", "bfloat16", "int32", "uint16", "uint8"
SB = (9, 8, 7)
SLOTS = NJ + 1
GW = 72 * SLOTS + 72
CE, CC, CT, CZ = 0, 512, 640, 768

SCRATCH = {"ps": ("psum", [128, 4096], F32)}


def _sb(dtype, **names):
    for n, w in names.items():
        SCRATCH[n] = ("sbuf", [128, w], dtype)


_sb(BF, x0=4 * C, X=1600, ub=512, vb=512, nega=512, negb=512, cb=4 * 768, G=4 * GW, m4=C, m16=C, junk=4 * C,
    FS=4 * C, A5=448, Et=512, Vt=512, DE=448, CV=448)
_sb(F32, r4=C, r16=C, pflt=8, ic=C, I=C, dmy=K, cs=96, yl=NJ, ya=NJ, yb=NJ, yc=28, yd=28, wr=C,
    z=C, zs=C, zz=144, KK=2 * C, M1=K, OE=C, sg=C, Vr=C, Rs=NJ, R2=NJ, rk=NJ, PL=C, am=C, rl=480, Bx=292, TAG=C,
    T1=C, T2=C, T3=C, T4=C, Q1=C, Q2=C, Q3=C, Q4=C, P1=K, P2=K, P3=K, P4=K, w=K, w1=K, wE=K, FQ=448, eqn=K, sel=28, lqf=K,
    q0=K, q1=K, q4=K, yo=C)
_sb(I32, rvt=NJ, pint=8, yi=NJ, yj=NJ, oi1=C, oi=C, qi=28, qj=28, qz=K)
_sb(U16, rvl=NJ, sOM=16, lOE=NJ, lp18=NJ, lp7=8, lpo=8, Bo=K, Lo=8, lrv=NJ, lrq=8, lA=28, rkl=NJ, Bp=C, L1=NJ, L2=NJ, L3=NJ, L4=NJ, lo=72,
    Pp=K, lE=28, lQ=28, lX=28, pls=40 * ROUNDS, pll=40 * ROUNDS)
for _n, _w in [("qx", C), ("qu", 128), ("qv", 128), ("uo", 128), ("um", 128), ("wq", 512), ("cq", 768), ("gq", GW), ("vq", 128),
               ("eq", 128 * ROUNDS), ("le", 128 * ROUNDS)]:
    SCRATCH[_n] = ("sbuf", [128, _w], CODE)
    SCRATCH[_n + "s"] = ("sbuf", [128, _w], U8)

QS = {"v": "qsv", "a": "qsa", "t": "qst", "g": "qsg"}
DS = ["dx", "du", "dv", "drv", "dwc", "dws", "dz", "dT1", "dL2", "dL3", "dLo", "dL4", "dP", "dlq", "doc", "dy"]
SEMAPHORES = list(QS.values()) + DS + ["rl"] + ["ap%d" % _t for _t in range(ROUNDS)] + ["ae%d" % _t for _t in range(ROUNDS)]


def make_tracker(g, T):
    eng = {"v": g.vector, "a": g.scalar, "t": g.tensor, "g": g, "s": g.sync}
    clk = {q: {} for q in eng}
    cnt = {}
    snaps = {}
    acc = {}
    seq = [0]

    def hit(a, b):
        if a[1] >= b[2] or b[1] >= a[2] or a[3] >= b[4] or b[3] >= a[4]:
            return False
        return not (a[5] == b[5] and a[5] > 1 and (a[3] - b[3]) % a[5])

    def bank(r):
        return (r[0], 0, 128, r[3] // 512 * 512, (r[4] + 511) // 512 * 512, 1) if r[0] == "ps" else r

    def merge(q, sem, val):
        own = clk[q]
        own[sem] = max(own.get(sem, 0), val)
        for v, s in snaps.get(sem, []):
            if v <= val:
                for a, b in s.items():
                    own[a] = max(own.get(a, 0), b)

    def emit(q, call, outs, ins, dma=None, remote=False):
        need = {}

        def want(rec):
            sem, val, order = rec[2], rec[3], rec[4]
            if clk[q].get(sem, 0) >= val:
                return
            if sem in DS:
                val = cnt[sem]
            if need.get(sem, (0, 0))[0] < val:
                need[sem] = (val, order)
        for r0 in ins:
            r = bank(r0)
            for rec in acc.get(r[0], []):
                if hit(r, rec[0]) and (rec[1] or (r[0] == "ps" and rec[5] != q)):
                    want(rec)
        for r0 in outs:
            r = bank(r0)
            for rec in acc.get(r[0], []):
                if hit(r, rec[0]) and not (rec[5] == q == "t"):
                    want(rec)
        for sem, (val, order) in sorted(need.items(), key=lambda e: -e[1][1]):
            if clk[q].get(sem, 0) < val:
                eng[q].wait_ge(T.sem[sem], val)
                merge(q, sem, val)
        made = call()
        seq[0] += 1
        if remote:
            return
        sem = dma or QS[q]
        cnt[sem] = cnt.get(sem, 0) + (16 if dma else 1)
        made.then_inc(T.sem[sem], 16 if dma else 1)
        snaps.setdefault(sem, []).append((cnt[sem], dict(clk[q])))
        for r0, wr in [(r, True) for r in outs] + [(r, False) for r in ins]:
            r = bank(r0)
            lst = acc.setdefault(r[0], [])
            if wr:
                lst[:] = [e for e in lst if not (e[0][1] >= r[1] and e[0][2] <= r[2] and e[0][3] >= r[3] and e[0][4] <= r[4] and r[5] == 1)]
            lst.append((r, wr, sem, cnt[sem], seq[0], q, dma))

    def arrive(regs, sem, val):
        seq[0] += 1
        for r in regs:
            acc.setdefault(r[0], []).append((r, True, sem, val, seq[0], "r", sem))

    def finish(extra):
        for sem in list(cnt):
            if clk["g"].get(sem, 0) < cnt[sem]:
                g.wait_ge(T.sem[sem], cnt[sem])
                merge("g", sem, cnt[sem])
        for sem, val in extra:
            if clk["g"].get(sem, 0) < val:
                g.wait_ge(T.sem[sem], val)
    return emit, arrive, finish


def rank_program(g, core, T, topo):
    rank = T.rank_of(core)
    if rank is None:
        return
    N = len(T.cores)
    nxt, prv = T.cores[(rank + 1) % N], T.cores[(rank - 1) % N]
    A, AF = AluOpType, ActivationFunctionType
    emit, arrive, finish = make_tracker(g, T)

    def W(n, c0=0, c1=None, s=1, p0=0, p1=128):
        return (n, p0, p1, c0, c1 if c1 is not None else (SCRATCH[n][1][1] if n in SCRATCH else T[n].shape[1]), s)

    def ap(r):
        if len(r) == 2:
            return ap(r[0]).indirect(ap(r[1]))
        n, p0, p1, c0, c1, s = r
        return T[n][p0:p1, c0:c1] if s == 1 else T[n][p0:p1, c0:c1:s]

    def by(r):
        return ap(r).bitcast(dt.uint8)

    def rg(*rs):
        o = []
        for r in rs:
            o += list(r) if len(r) == 2 else [r]
        return o

    def ind(win, off):
        return (win, off)

    def tt(out, a, b, op):
        emit("v", lambda: g.vector.tensor_tensor(ap(out), ap(a), ap(b), op), rg(out), rg(a, b))

    def ts(out, a, s1, op0, s2=None, op1=None):
        x1, x2 = (ap(s) if isinstance(s, tuple) else s for s in (s1, s2))
        sc = [s for s in (s1, s2) if isinstance(s, tuple)]
        if op1 is None:
            emit("v", lambda: g.vector.tensor_scalar(ap(out), ap(a), x1, None, op0), rg(out), rg(a, *sc))
        else:
            emit("v", lambda: g.vector.tensor_scalar(ap(out), ap(a), x1, x2, op0, op1), rg(out), rg(a, *sc))

    def cp(out, a):
        emit("v", lambda: g.vector.tensor_copy(ap(out), ap(a)), rg(out), rg(a))

    def scatter(win, off, a):
        emit("v", lambda: g.vector.tensor_copy(ap((win, off)), ap(a)), [win], [off, a])

    def fill(out, val):
        emit("v", lambda: g.vector.memset(ap(out), val), rg(out), [])

    def scan(out, d0, d1, init, op0, op1):
        emit("v", lambda: g.vector.tensor_tensor_scan(ap(out), ap(d0), ap(d1), init, op0, op1), [out], [d0, d1])

    def act(out, a, fn, scale=1.0, bias=0.0, accum=None):
        kw, ins, outs = {}, rg(a), rg(out)
        if scale != 1.0:
            kw["scale"] = scale
        if isinstance(bias, tuple):
            kw["bias"] = ap(bias)
            ins.append(bias)
        elif bias != 0.0:
            kw["bias"] = bias
        if accum is not None:
            kw["accum_out"] = ap(accum)
            outs.append(accum)
        emit("a", lambda: g.scalar.activation(ap(out), ap(a), fn, **kw), outs, ins)

    def iota(out, pattern, base=0, cm=0):
        kw = {} if SCRATCH[out[0]][2] == I32 else {"allow_small_or_imprecise_dtypes": True}
        emit("g", lambda: g.iota(ap(out), pattern, base, cm, **kw), rg(out), [])

    def asel(out, a, pattern, op, base, cm):
        emit("g", lambda: g.affine_select(ap(out), ap(a), pattern, op, 0.0, base, cm), rg(out), rg(a))

    def dma(q, sem, out, a, o8=False, a8=False):
        e = {"s": g.sync, "a": g.scalar}[q]
        emit(q, lambda: e.dma_start(by(out) if o8 else ap(out), by(a) if a8 else ap(a)), rg(out), rg(a), dma=sem)

    def rows_on(q, sem, out, o0, o1, src, n, d):
        for p0, p1, to in ((0, 128 - 16 * d, 16 * d), (128 - 16 * d, 128, 0)):
            if p0 < p1:
                o, a = W(out, o0, o1, p0=to, p1=to + p1 - p0), W(src, p0=p0, p1=p1)
                e = {"s": g.sync, "a": g.scalar}[q]
                emit(q, lambda: e.dma_start(ap(o), T[src][p0:p1:16, 0:n]), [o], [a], dma=sem)

    def quant(n, c0, c1, src):
        o, s = W(n, c0, c1), W(n + "s", c0, c1)
        emit("v", lambda: g.vector.quantize_mx(ap(o), ap(s), ap(src)), rg(o, s), rg(src))

    def mm(bank, wn, w0, xn, x0, n, start=True, stop=True):
        o = W("ps", 512 * bank, 512 * bank + n)
        w, ws, x, xs = W(wn, w0, w0 + 128), W(wn + "s", w0, w0 + 128), W(xn, x0, x0 + n), W(xn + "s", x0, x0 + n)
        emit("t", lambda: g.tensor.matmul_mx(ap(o), ap(w), ap(ws), ap(x), ap(xs), start, stop), rg(o), rg(w, ws, x, xs))

    def bk(b, c0, c1):
        return W("ps", 512 * b + c0, 512 * b + c1)

    def pick(out, off):
        emit("v", lambda: g.vector.tensor_copy(ap(W(out)).bitcast(dt.uint32), ap(W("qu")).bitcast(dt.uint32).indirect(ap(off))), [W(out)], [W("qu"), off])
        emit("a", lambda: g.scalar.activation(ap(W(out + "s")), ap(W("qus")).indirect(ap(off)), AF.Copy), [W(out + "s")], [W("qus"), off])

    LF, LH, LB, LHE, LP, LZ, LBZ = (W("pflt", i, i + 1) for i in range(7))
    PI, LI, LHI, LBI, LPI, LPJ = (W("pint", i, i + 1) for i in range(6))
    C8, C28, C16, KC = W("cs", 0, 8), W("cs", 32, 60), W("cs", 32, 32 + NJ), W("cs", 64, 64 + NJ)
    B16, B4 = W("KK", 0, C), W("KK", C, 2 * C)

    def last(out, a, keep):
        scan(out, keep, a, 0.0, A.mult, A.add)

    def to28(row, tmp, out):
        scan(tmp, row, W("M1"), 1.0, A.min, A.add)
        ts(out, (tmp[0], 0, 128, 3, K, 4), 4 * UNIT, A.mult, LBZ, A.add)

    dma("s", "du", W("ub"), W("u"))
    dma("a", "dx", W("x0"), W("x"))
    dma("a", "drv", W("rvt"), W("rv"))
    dma("s", "dwc", W("wq"), W("wc"), o8=True)
    dma("s", "dws", W("wqs"), W("ws"))
    dma("s", "dv", W("vb"), W("v"))

    iota(PI, [[0, 1]], 0, 1)
    iota(C8, [[16, 8]])
    iota(W("ic"), [[1, C]])
    iota(C28, [[16, 28]])
    iota(W("r16"), [[0, NJ], [1, 16]])
    iota(W("r4"), [[0, 72], [1, 4]])
    iota(KC, [[-16, NJ]], C - 1)
    fill(W("nega"), -1.0)
    ts(LI, PI, 15, A.bitwise_and)
    cp(W("sOM", 0, 8), C8)
    ts(W("sOM", 8, 16), C8, 8.0, A.add)
    cp(LF, LI)
    ts(LHI, LI, 2, A.logical_shift_right)
    ts(LBI, LI, 3, A.bitwise_and)
    for s in range(1, 9):
        fill(W("G", 288 * s + 288 - 16 * s, 288 * s + 288), 0.0)
    asel(W("negb"), W("nega"), [[-16, 8], [0, 64]], A.is_ge, 0, 1)
    asel(W("negb"), W("negb"), [[16, 8], [0, 64]], A.is_ge, 15, -1)
    asel(W("cb", 4 * CC, 4 * CC + 512), W("negb"), [[0, 32], [1, 4], [-1, 4]], A.is_equal, 0, 0)
    asel(W("cb", 4 * CT, 4 * CT + 512), W("cb", 4 * CC, 4 * CC + 512), [[1, 128], [0, 4]], A.is_ge, -1, -1)
    for b in range(4):
        asel(W("cb", 512 * b, 512 * b + 512), W("nega"), [[-1, 512]], A.is_equal, b, 4)
    for n in ("Et", "Vt"):
        asel(W(n, 448, 512), W("nega", 0, 64), [[0, 64]], A.is_ge, -1, 0)
    iota(W("w", K - 1, K), [[0, 1]])
    cp(LH, LHI)
    cp(LB, LBI)
    ts(LPI, PI, 3.0 * 4, A.add)
    ts(W("yl"), C16, LF, A.add)
    ts(W("lOE"), C16, 15.0, A.add)
    ts(LPJ, LPI, 2, A.logical_shift_right)
    ts(W("ya"), W("yl"), -8.5, A.add, 1.0 / 18, A.mult)
    ts(W("yd", 0, NJ), W("yl"), -3.0, A.add, 1.0 / 7, A.mult)
    ts(LPI, LPJ, 3, A.bitwise_and)
    cp(W("yi"), W("ya"))
    cp(W("yj"), W("yd", 0, NJ))
    ts(W("ya"), W("yl"), 16.0, A.mult)
    ts(W("m16"), W("r16"), LF, A.is_equal)
    fill(W("pls"), 0)
    cp(W("rvl"), W("rvt"))
    act(W("yo"), W("ic"), AF.Relu, bias=-1.0)
    act(W("I"), W("ic"), AF.Copy, scale=1.0 / UNIT)
    act(W("T3"), W("yo"), AF.Identity, scale=-1.0 / UNIT, bias=(C - 1) / UNIT)
    act(B16, W("r16"), AF.Sign)
    act(B4, W("r4"), AF.Sign)
    quant("qu", 0, 128, W("ub"))
    pick("uo", W("sOM", 0, 8))

    def consts_first():
        pick("um", W("sOM", 8, 16))
        ts(W("m4"), W("r4"), LH, A.is_equal)
        for s in list(range(9, NJ)) + [SLOTS]:
            act(W("G", 288 * s, 288 * s + 288), W("ic"), AF.Copy, scale=0.0)

    def consts_count():
        ts(W("yb"), W("yi"), -287.0, A.mult)
        ts(W("yd", 0, NJ), W("yj"), -111.0, A.mult)
        ts(W("lrv"), W("yl"), -1.0, A.mult, float(C - 1), A.add)
        ts(LHE, LH, 8.0, A.mult)
        cp(LP, LPI)
        ts(LZ, LH, 0.0, A.is_equal, -4.0 * UNIT, A.mult)
        ts(W("yc"), C28, 2.0, A.mult, 4.0, A.add)
        ts(W("lrq", 0, 7), W("yl", 0, 7), -1.0, A.mult, float(K - 1), A.add)
        ts(W("M1"), W("r4", 0, K), LP, A.is_equal)
        tt(LBZ, LZ, LB, A.add)
        ts(W("yc"), W("yc"), LHE, A.add)
        ts(W("lA"), W("yc"), LB, A.add)
        quant("cq", CC, CZ, W("cb", 4 * CC, 4 * CZ))
        tt(W("yb"), W("yb"), W("ya"), A.add)
        tt(W("yd", 0, NJ), W("yd", 0, NJ), W("ya"), A.add)
        fill(W("Rs", 0, 1), 0.0)
        cp(W("lp18"), W("yb"))
        cp(W("lp7", 0, 7), W("yd", 0, 7))
        ts(W("lpo", 0, 7), W("yd", 0, 7), 2.0, A.mult, 1.0, A.add)
        fill(W("Bx", 0, 1), 0.0)

    def pads():
        for t in range(ROUNDS):
            dma("s", "dz", W("le", 128 * t + K, 128 * t + 128), W("eq", K, 128), o8=True, a8=True)
            dma("s", "dz", W("les", 128 * t + K, 128 * t + 128), W("eqs", K, 128))

    ne, np_ = len(topo.engines(core, nxt)[:8]), len(topo.engines(prv, core)[:8])
    emask = sum(1 << e for e in topo.engines(core, nxt)[:8])
    rid, pid = topo.addr(nxt, core)
    rlc = [0]

    def send(out_ap, src, in_ap, sem):
        emit("g", lambda: g.remote_dma(out_ap, in_ap, T.sem[sem], T.sem.rl, pid, rid, emask), [], [src], remote=True)
        rlc[0] += ne

    for t in range(ROUNDS):
        quant("qx", 0, C, W("x0") if t == 0 else W("X", 0, 4 * C))
        if t == 0:
            consts_first()
        mm(0, "uo", 0, "qx", 0, C)
        mm(1, "um", 0, "qx", 0, C)
        mm(7, "uo", 0, "qx", 0, C)
        So = bk(0, 0, C)
        tt(W("z"), So, W("m16"), A.mult)
        act(W("sg"), bk(1, 0, C), AF.Sign)
        last(W("zs"), W("z"), B16)
        act(W("sg"), W("sg"), AF.Sign, bias=-0.5)
        for j in SB:
            r = 160 * (j - SB[-1])
            act(W("rl", r, r + 16 * j + 16), bk(7, 0, 16 * j + 16), AF.Relu, scale=-1.0, bias=W("zs", 16 * j + 15, 16 * j + 16))
        for j in SB:
            s, r = 288 * (NJ - 1 - j), 160 * (j - SB[-1])
            act(W("G", s, s + 16 * j), W("rl", r, r + 16 * j), AF.Sign, accum=W("Rs", j, j + 1))
            act(W("G", s + 16 * j, s + 16 * j + 16), W("rl", r + 16 * j, r + 16 * j + 16), AF.Sign)
        act(W("OE"), ind(W("zs"), W("lOE")), AF.Copy)

        def chunk(k, n):
            quant("gq", 288 * k, 288 * k + 72 * n, W("G", 1152 * k, 1152 * k + 288 * n))
            n = min(n, SLOTS - 4 * k)
            for s in range(max(4 * k - 1, 0), 4 * k + n - (n == 4)):
                mm(6, "cq", CT if s == NJ else CC, "gq", 72 * s, 128, start=(s == 0), stop=(s == NJ))
        for s in range(SLOTS):
            if s % 4 == 1 and s > 1:
                if t == 0 and s == 5:
                    consts_count()
                chunk(s // 4 - 1, 4)
            j = NJ - 1 - s
            if j < 0:
                tt(W("G", 288 * s, 288 * s + 288), So, W("OE"), A.is_equal)
            elif j not in SB:
                ts(W("G", 288 * s, 288 * s + 16 * j + 16), bk(0, 0, 16 * j + 16), W("zs", 16 * j + 15, 16 * j + 16), A.is_lt)
                if j:
                    act(W("junk", 288 * (s % 4), 288 * (s % 4) + 16 * j), W("G", 288 * s, 288 * s + 16 * j), AF.Copy, accum=W("Rs", j, j + 1))
        chunk(4, 4 if t == 0 else 3)
        if t == 0:
            act(W("T4"), ind(W("T3"), W("rvl")), AF.Copy)
            act(W("wr"), ind(W("T4"), W("lrv")), AF.Copy)
        tt(W("Vr"), W("sg"), W("I"), A.add)
        tt(W("zz", 0, 72), bk(6, 0, 72), W("m4", 0, 72), A.mult)
        last(W("zz", 72, 144), W("zz", 0, 72), W("KK", C, C + 72))
        tt(W("R2"), W("Rs"), KC, A.add)
        tt(W("rk"), W("zz", 75, 144, 4), W("R2"), A.add)
        cp(W("rkl"), W("rk"))
        scatter(W("PL"), W("rkl"), W("Vr"))
        tt(W("am"), W("PL"), W("wr"), A.min)
        scan(W("Bx", 1, C + 1), W("am"), W("am"), 0.0, A.max, A.max)
        dma("s", "dT1", W("T1", p0=16), W("Bx", 0, C, p1=112))
        dma("s", "dT1", W("T1", p1=16), W("Bx", 0, C, p0=112))
        ts(W("Bp"), ind(W("Bx", 0, C), W("lp18")), UNIT, A.mult)
        rows_on("s", "dL2", "L2", 0, NJ, "Bp", C, 2)
        rows_on("s", "dL3", "L3", 0, NJ, "Bp", C, 3)
        ts(W("Bo"), ind(W("Bx", 0, C), W("lpo", 0, 7)), UNIT, A.mult)
        rows_on("s", "dLo", "Lo", 0, 7, "Bo", K, 4)
        rows_on("s", "dL4", "L4", 0, NJ, "Bp", C, 4)
        rows_on("s", "dL4", "L1", 0, NJ, "Bp", C, 1)
        if t == 0:
            quant("cq", CE, CC, W("cb", 0, 4 * CC))
        for b in range(4):
            mm(2 + b, "cq", 128 * b, "qx", 0, C)
        for b in range(4):
            act(W("X", b, 4 * C, 4), bk(2 + b, 0, C), AF.Copy, scale=-1.0)
        ts(W("oi1"), W("PL"), UNIT, A.mult, UNIT, A.add)
        ts(W("oi"), W("oi1"), 1023, A.bitwise_and)
        tt(W("z"), W("oi"), W("m4"), A.mult)
        last(W("zs"), W("z"), B4)
        ts(W("lo"), W("zs", 3, C, 4), 4.0, A.mult, LB, A.add)
        act(W("FS"), ind(W("X", 0, 4 * C), W("lo")), AF.Copy, scale=2.0 ** -5)
        act(W("A5"), ind(W("FS"), W("lA")), AF.Copy)
        odd = [(n, 0, 128, 1, 2 * K, 2) for n in ("T1", "T2", "T3")]
        tt(W("P1"), odd[0], W("I", 1, 2 * K, 2), A.max)
        cp(W("T2"), ind(W("T1"), W("L2")))
        cp(W("T3"), ind(W("T2"), W("L3")))
        tt(W("P2"), odd[1], W("P1"), A.max)
        tt(W("P3"), odd[2], W("P2"), A.max)
        tt(W("P4"), ind(W("T3"), W("Lo", 0, 7)), W("P3"), A.max)
        ts(W("Pp"), ind(W("P4"), W("lp7", 0, 7)), UNIT, A.mult)
        o = 40 * t
        for d in range(5):
            rows_on("sa"[d % 2], "dP", "pls", o + 8 * d, o + 8 * d + 7, "Pp", K, d)
        to28(W("P4"), W("wE"), W("lE"))
        tt(W("Et", 0, 448), ind(W("FS"), W("lE")), W("A5"), A.add)
        quant("eq", 128 * t, 128 * t + 128, W("Et"))
        if t == 0:
            pads()
        pl, plo = W("pls", o, o + 40), W("pll", o, o + 40)
        e, eo = W("eq", 128 * t, 128 * t + K), W("le", 128 * t, 128 * t + K)
        send(by(eo), e, by(e), "ae%d" % t)
        send(ap(plo), pl, ap(pl), "ap%d" % t)
        es, eso = W("eqs", 128 * t, 128 * t + K), W("les", 128 * t, 128 * t + K)
        send(ap(eso), es, ap(es), "ae%d" % t)
        if t == 0:
            act(W("T3", 0, K), W("ic", 0, K), AF.Identity, bias=float(C))
            tt(W("dmy"), W("T3", 0, K), W("m4", 0, K), A.mult)
        ts(W("yo"), W("oi"), 1.0 / (TAGU * UNIT), A.mult)
        tt(W("TAG"), W("yo"), W("I"), A.add)
        act(W("Q1"), ind(W("TAG"), W("L1")), AF.Copy)
        for d in (2, 3, 4):
            act(W("Q%d" % d), ind(W("Q%d" % (d - 1)), W("L%d" % d)), AF.Copy)
        arrive([plo], "ap%d" % t, np_)
        arrive([eo, eso], "ae%d" % t, 2 * np_)
        for b in range(4):
            mm(2 + b, "cq", 128 * b, "le", 128 * t, 128)
        for b in range(4):
            act(W("DE", b, 448, 4), bk(2 + b, 0, K), AF.Copy, scale=-0.5)
        cp(W("q0"), ind(W("Q1"), W("pll", o + 8, o + 15)))
        tt(W("q1"), ind(W("TAG"), W("pll", o, o + 7)), W("q0"), A.max)
        tt(W("q0"), ind(W("Q2"), W("pll", o + 16, o + 23)), W("q1"), A.max)
        tt(W("q1"), ind(W("Q3"), W("pll", o + 24, o + 31)), W("q0"), A.max)
        tt(W("q4"), ind(W("Q4"), W("pll", o + 32, o + 39)), W("q1"), A.max)
        to28(W("q4"), W("wE"), W("lQ"))
        tt(W("Vt", 0, 448), ind(W("FS"), W("lQ")), W("DE"), A.add)
        act(W("FQ"), ind(W("FS"), W("lQ")), AF.Copy, scale=32.0)
        quant("vq", 0, 128, W("Vt"))
        hb = (0, 1, 6, 7)
        for b in range(4):
            mm(hb[b], "wq", 128 * b, "vq", 0, 128)
        tt(W("eqn", 0, K - 1), W("q4", 0, K - 1), W("q4", 1, K), A.is_equal)
        ts(W("qi"), W("wE", 3, K, 4), TAGU * UNIT, A.mult)
        tt(W("w", 0, K - 1), W("eqn", 0, K - 1), W("dmy", 0, K - 1), A.mult)
        ts(W("qj"), W("qi"), 511, A.bitwise_and)
        last(W("w1"), W("w"), W("KK", C, C + K))
        for b in range(3):
            tt(W("CV", b, 448, 4), bk(hb[b], 0, K), W("FQ", b, 448, 4), A.add)
        tt(W("sel"), W("qj"), W("w1", 3, K, 4), A.max)
        tt(W("CV", 3, 448, 4), bk(hb[3], 0, K), W("FQ", 3, 448, 4), A.add)
        ts(W("lX"), W("sel"), 4.0, A.mult, LB, A.add)
        scatter(W("X"), W("lX"), W("CV"))
        if t == 0:
            quant("qv", 0, 128, W("vb"))
    quant("qx", 0, C, W("X", 0, 4 * C))
    mm(0, "qv", 0, "qx", 0, C)
    emit("s", lambda: g.sync.dma_start(T.oc[:, :], by(W("qx"))), [], [W("qx")], dma="doc")
    ts(W("qz"), ind(W("q4"), W("lrq", 0, 7)), UNIT, A.mult)
    act(W("yo"), bk(0, 0, C), AF.Copy)
    ts(W("lqf"), W("qz"), -1.0, A.mult, float(C - 1), A.add)
    emit("a", lambda: g.scalar.dma_start(T.y[:, :], T.yo[:, :]), [], [W("yo")], dma="dy")
    for k in range(4):
        emit("s", lambda: g.sync.dma_start(T.osc[4 * k:4 * k + 4, :], T.qxs[32 * k:32 * k + 4, 0:C]), [], [W("qxs")], dma="doc")
    emit("s", lambda: g.sync.dma_start(T.lq[:, :], T.lqf[0:128:16, 0:K]), [], [W("lqf")], dma="dlq")
    finish([("rl", rlc[0])] + [("ap%d" % t, np_) for t in range(ROUNDS)] + [("ae%d" % t, 2 * np_) for t in range(ROUNDS)])
